import numpy as np, ml_dtypes
CORES = [22,38,54,62,70,110,23,39,55,63,71,111]
N = 12
TOK, K, FT = 512, 3, 1
ROUTE = [[[2,3,10],[6,7,10],[4,10,11],[2,8,9],[4,5,11],[3,10,11],[1,7,10],[5,6,8],[1,4,7],[1,3,8],[1,6,9],[2,8,10],[3,8,10],[1,5,7],[4,8,9],[1,7,8],[3,5,9],[0,5,11],[7,10,11],[5,8,9],[6,8,11],[1,3,11],[4,6,8],[4,8,10],[5,10,11],[1,4,8],[4,5,6],[5,6,9],[4,8,9],[4,5,7],[4,6,10],[2,6,7],[0,8,9],[1,4,5],[3,9,10],[4,8,10],[1,4,9],[4,9,10],[2,7,9],[1,4,11],[6,7,9],[1,8,9],[2,9,10],[0,7,10],[0,6,8],[1,7,8],[0,3,10],[1,4,9],[4,7,8],[1,4,11],[8,9,11],[7,8,11],[6,9,10],[4,5,8],[0,5,11],[0,2,9],[4,5,10],[7,8,11],[0,8,11],[5,8,10],[4,5,6],[4,5,7],[1,8,11],[3,4,8],[0,4,5],[3,9,11],[3,6,8],[0,1,2],[2,5,9],[4,9,10],[1,4,8],[3,4,7],[5,8,10],[0,2,10],[6,7,11],[1,8,9],[2,4,7],[5,7,11],[7,9,10],[7,9,10],[0,4,6],[7,9,10],[2,6,9],[0,3,7],[3,7,9],[2,9,11],[1,3,10],[3,5,11],[2,7,10],[5,8,10],[0,7,10],[1,6,10],[1,3,7],[1,7,11],[4,6,7],[0,1,8],[1,2,7],[0,6,11],[1,4,7],[3,6,8],[1,6,7],[5,8,10],[6,8,9],[1,3,11],[2,6,9],[3,4,11],[5,7,9],[0,4,9],[4,8,10],[2,5,6],[9,10,11],[1,8,10],[0,3,10],[1,3,4],[1,3,10],[1,6,7],[0,2,5],[4,9,11],[3,7,11],[1,8,11],[3,4,7],[7,8,11],[1,7,10],[1,4,8],[1,2,9],[1,4,11],[1,7,10],[2,10,11],[1,4,7],[1,7,8],[6,8,9],[4,10,11],[2,5,8],[5,6,9],[2,5,6],[4,8,10],[1,7,9],[1,5,7],[0,3,7],[4,6,8],[5,9,11],[0,5,7],[2,8,11],[0,2,5],[4,6,8],[4,5,8],[5,6,9],[3,5,9],[1,6,7],[0,4,5],[1,5,10],[2,3,10],[1,3,8],[2,4,8],[2,6,9],[5,6,10],[5,6,8],[1,5,8],[3,6,9],[1,2,11],[1,10,11],[0,8,9],[0,2,10],[0,8,9],[5,9,11],[2,5,11],[1,5,6],[2,5,8],[2,5,7],[1,6,11],[6,8,9],[0,4,6],[2,3,9],[4,6,8],[4,5,8],[3,8,9],[3,4,11],[3,6,8],[0,8,11],[3,5,11],[2,9,11],[7,9,11],[4,6,7],[3,4,7],[0,3,5],[7,8,11],[0,2,7],[1,4,9],[0,7,9],[4,9,10],[3,4,7],[1,7,10],[7,10,11],[3,9,11],[1,7,9],[4,7,9],[3,4,11],[7,8,9],[0,6,11],[0,2,6],[2,3,9],[0,7,10],[2,3,8],[1,3,10],[0,4,7],[5,6,9],[5,7,10],[3,8,9],[0,1,5],[7,8,11],[3,5,8],[4,8,11],[3,7,11],[3,5,9],[3,4,10],[0,7,10],[0,1,9],[2,3,7],[3,5,11],[1,3,4],[4,7,9],[4,8,9],[0,6,7],[2,4,10],[1,2,7],[1,3,8],[1,4,7],[1,5,7],[0,1,6],[4,8,9],[1,2,11],[5,8,9],[4,5,7],[2,8,9],[6,7,10],[0,7,9],[3,8,11],[1,4,9],[1,4,10],[0,7,8],[1,5,7],[2,3,5],[2,5,6],[3,7,10],[6,7,8],[0,3,7],[2,3,8],[2,8,11],[0,1,8],[0,3,10],[0,6,9],[0,6,11],[6,10,11],[1,3,7],[0,2,8],[3,4,11],[3,10,11],[2,9,11],[4,8,11],[0,3,6],[0,4,11],[0,3,5],[0,8,11],[3,7,9],[1,6,7],[2,3,10],[3,6,11],[1,3,9],[1,4,7],[2,6,8],[1,3,6],[1,7,10],[0,1,4],[0,1,4],[7,8,11],[1,6,11],[0,8,9],[5,7,9],[4,5,8],[2,5,9],[0,8,11],[1,5,9],[1,7,9],[4,8,9],[0,4,6],[0,8,10],[1,2,5],[7,8,10],[7,9,10],[2,5,11],[4,7,9],[1,2,11],[0,5,11],[3,4,8],[0,3,7],[1,4,10],[1,3,9],[3,8,9],[6,7,8],[1,2,10],[0,3,8],[3,6,7],[0,9,10],[2,6,11],[0,7,8],[1,9,11],[1,8,11],[0,4,9],[8,9,10],[1,8,11],[2,5,10],[2,9,11],[0,9,11],[3,7,9],[0,2,3],[5,6,7],[3,5,7],[3,5,10],[2,4,10],[0,4,5],[3,5,9],[0,2,7],[6,7,10],[1,9,10],[1,2,11],[3,4,11],[0,3,10],[3,5,11],[0,2,7],[0,5,11],[7,8,9],[4,7,9],[3,5,11],[3,5,11],[1,3,9],[3,6,8],[0,1,3],[0,1,2],[4,7,8],[1,4,11],[0,1,8],[1,7,11],[2,3,4],[2,7,8],[5,6,9],[7,9,11],[5,6,10],[2,5,7],[2,6,11],[2,3,10],[1,4,5],[1,10,11],[1,3,4],[0,1,10],[2,3,10],[1,5,6],[1,2,7],[1,2,11],[4,6,11],[0,1,10],[0,7,8],[3,8,11],[0,2,10],[4,6,8],[2,3,8],[1,3,8],[1,4,10],[3,6,9],[2,7,11],[0,5,7],[2,7,11],[5,7,9],[5,6,9],[0,4,11],[1,2,9],[0,4,11],[1,7,10],[5,6,7],[3,6,11],[1,4,10],[1,2,6],[0,1,2],[3,4,8],[0,2,8],[0,6,7],[1,3,6],[1,2,11],[6,8,9],[0,9,11],[1,9,10],[4,9,10],[0,2,7],[1,4,10],[1,7,10],[0,1,9],[9,10,11],[1,5,9],[2,5,7],[2,3,6],[5,6,10],[4,9,11],[4,8,10],[2,4,6],[1,4,7],[4,8,10],[0,3,9],[5,10,11],[2,3,10],[5,7,10],[0,8,11],[2,5,7],[1,2,11],[2,5,11],[2,4,6],[2,6,7],[0,4,11],[5,9,10],[1,6,7],[0,4,8],[0,10,11],[0,1,8],[4,6,8],[2,3,5],[4,7,8],[1,9,11],[4,6,7],[0,7,10],[0,2,9],[2,5,10],[0,3,8],[0,1,5],[1,3,5],[2,3,5],[0,10,11],[0,5,9],[0,4,6],[6,9,11],[0,4,7],[1,3,7],[2,7,10],[1,2,4],[5,9,10],[1,3,10],[0,1,11],[2,8,10],[1,5,8],[6,7,11],[2,7,10],[1,5,10],[4,7,9],[0,1,10],[4,5,10],[2,4,11],[1,8,10],[4,6,11],[0,6,8],[4,10,11],[1,3,9],[0,7,11],[1,6,9],[3,9,10],[7,8,9],[1,3,11],[0,6,11],[5,8,10],[3,5,7],[2,6,9],[1,3,4],[3,4,7],[3,6,9],[6,8,9],[2,4,11],[0,1,6],[2,4,7],[0,3,10],[0,7,10],[0,4,9],[1,6,9],[4,9,10],[2,3,11],[1,4,6],[0,1,5],[0,2,4],[1,8,10],[0,6,11],[1,3,8],[2,4,7],[1,9,11],[2,3,8],[5,6,8],[0,3,10],[7,10,11],[1,5,6],[0,6,9],[0,3,10],[3,8,11],[2,4,10],[1,5,10],[3,5,11],[4,10,11],[2,6,11],[2,5,6],[4,5,11],[5,8,10],[7,9,10],[3,6,10],[3,4,8],[4,6,11],[6,9,10],[1,2,10],[2,6,7],[1,5,11]],[[4,7,8],[0,3,7],[4,6,7],[3,6,7],[3,4,6],[0,3,5],[7,8,10],[0,1,9],[0,4,7],[0,1,3],[2,3,7],[1,2,4],[1,4,10],[0,4,5],[5,9,10],[2,4,5],[5,8,11],[3,5,11],[3,4,9],[3,7,10],[0,1,10],[1,6,11],[1,3,11],[2,9,10],[0,4,5],[0,8,9],[4,5,8],[0,5,9],[2,4,11],[3,4,11],[0,2,9],[6,9,11],[9,10,11],[2,9,10],[4,7,11],[5,8,11],[4,6,8],[3,5,10],[3,6,10],[7,8,9],[0,1,3],[2,5,11],[2,4,8],[3,9,10],[0,6,11],[1,2,10],[0,8,11],[1,4,10],[1,7,10],[3,5,7],[1,3,10],[5,7,8],[0,3,10],[1,9,10],[0,1,7],[2,7,8],[4,6,10],[1,2,7],[8,9,11],[1,4,11],[2,6,11],[2,6,8],[2,5,11],[4,5,6],[0,4,9],[1,9,10],[4,9,11],[0,6,10],[1,7,9],[1,5,7],[0,1,8],[2,7,10],[1,7,9],[2,3,5],[4,5,10],[4,5,11],[6,9,10],[1,2,11],[2,8,9],[1,4,8],[3,5,11],[2,4,7],[6,7,11],[3,4,9],[7,8,11],[2,3,7],[2,6,10],[1,3,9],[5,9,10],[6,7,10],[2,3,5],[0,2,5],[0,3,5],[1,2,4],[0,5,7],[2,6,8],[4,7,8],[3,4,5],[3,4,9],[0,9,10],[2,7,8],[2,9,10],[1,5,8],[0,9,11],[0,5,8],[3,8,11],[5,6,11],[0,4,10],[2,8,9],[1,4,5],[2,4,7],[1,4,11],[0,6,7],[6,8,9],[0,2,6],[0,3,4],[1,8,11],[3,8,9],[1,2,8],[7,8,10],[2,5,7],[3,6,8],[0,1,8],[0,1,3],[3,5,11],[0,2,10],[4,9,11],[1,5,10],[1,5,10],[6,8,10],[5,7,11],[1,8,10],[1,8,10],[2,4,6],[0,5,7],[2,7,9],[3,7,9],[0,3,7],[6,7,8],[1,4,5],[5,7,9],[4,5,11],[2,6,9],[6,7,10],[2,3,8],[3,9,10],[2,4,6],[3,8,9],[4,5,7],[4,5,10],[2,7,11],[7,8,11],[1,7,8],[4,9,11],[0,3,11],[1,2,3],[0,5,9],[1,7,11],[3,6,11],[0,3,6],[2,4,6],[0,5,9],[5,7,10],[6,9,11],[1,7,9],[0,6,9],[2,4,10],[2,6,8],[2,4,7],[1,5,9],[1,10,11],[1,3,11],[3,8,10],[1,9,10],[3,4,11],[1,2,6],[0,6,11],[2,3,10],[1,3,5],[4,5,10],[1,9,11],[0,4,5],[2,8,10],[2,8,11],[1,8,9],[1,2,7],[6,8,9],[0,1,6],[4,5,10],[4,9,10],[0,2,3],[0,9,11],[1,9,10],[1,5,8],[1,5,6],[5,10,11],[5,6,9],[2,3,10],[8,10,11],[5,9,10],[1,7,11],[4,5,6],[0,9,11],[0,9,11],[4,6,8],[1,3,9],[0,3,5],[1,3,9],[1,8,9],[4,10,11],[2,4,10],[5,7,10],[1,4,8],[7,9,10],[4,6,10],[2,7,10],[2,4,11],[1,4,5],[1,8,9],[5,6,10],[4,7,11],[5,6,7],[5,6,7],[3,4,9],[0,4,11],[2,6,9],[1,2,6],[1,2,11],[5,6,8],[2,3,6],[3,4,5],[0,5,9],[2,4,7],[0,5,10],[0,9,10],[4,7,9],[1,5,11],[1,2,8],[0,7,8],[0,2,7],[2,4,5],[1,4,10],[1,5,9],[4,7,9],[0,2,6],[1,6,11],[3,4,6],[0,5,8],[4,8,10],[6,9,11],[0,4,9],[6,8,9],[0,8,10],[2,8,10],[5,7,8],[0,1,7],[0,8,9],[0,5,8],[3,6,11],[0,6,7],[1,5,9],[2,7,8],[2,10,11],[2,6,7],[5,10,11],[0,4,5],[9,10,11],[2,9,10],[1,2,5],[2,5,6],[1,7,11],[2,8,10],[1,3,6],[3,5,8],[0,7,9],[2,5,9],[0,7,11],[5,6,11],[4,9,10],[2,3,7],[2,4,11],[3,7,10],[0,9,11],[0,10,11],[5,7,11],[2,4,7],[1,3,7],[2,4,10],[2,3,10],[1,2,5],[9,10,11],[2,4,5],[0,10,11],[0,1,9],[0,1,11],[4,7,9],[0,9,11],[5,8,10],[0,5,11],[4,5,9],[1,5,11],[4,6,7],[6,7,11],[0,3,5],[5,7,9],[1,6,11],[1,3,10],[1,2,6],[6,8,10],[0,5,10],[6,7,9],[6,7,8],[4,6,11],[1,3,8],[5,6,8],[1,3,8],[0,4,6],[5,9,11],[2,3,4],[0,1,8],[2,3,7],[0,8,10],[3,10,11],[3,4,6],[0,8,10],[1,3,11],[3,4,6],[7,8,10],[1,8,11],[0,2,8],[1,6,7],[0,3,10],[3,5,9],[5,9,10],[2,3,8],[0,5,7],[1,2,5],[1,3,8],[3,7,10],[0,8,10],[2,3,4],[3,7,8],[0,1,5],[3,8,9],[1,3,7],[0,4,9],[1,7,10],[0,6,7],[5,8,11],[1,6,11],[3,9,10],[0,2,7],[5,9,10],[2,3,9],[0,3,6],[3,5,9],[0,3,9],[3,6,8],[1,2,5],[2,5,6],[4,5,11],[2,3,8],[1,4,7],[1,9,11],[9,10,11],[4,5,6],[7,8,9],[2,5,6],[1,6,7],[0,8,10],[5,7,10],[2,7,10],[1,4,8],[3,5,7],[6,9,10],[1,6,7],[2,9,10],[0,1,5],[0,1,5],[0,2,8],[1,8,11],[4,7,11],[1,3,11],[2,6,11],[1,5,11],[0,2,8],[1,6,7],[5,6,10],[4,6,11],[0,5,10],[6,9,11],[1,8,10],[0,7,9],[7,9,10],[8,10,11],[0,7,11],[0,2,8],[5,9,11],[0,2,8],[2,9,10],[0,1,11],[0,1,4],[0,10,11],[2,5,8],[2,6,10],[1,2,7],[0,3,10],[1,3,10],[0,5,7],[0,8,10],[3,7,11],[5,6,7],[0,8,9],[0,5,10],[2,4,11],[0,1,3],[6,8,10],[6,7,10],[2,7,10],[6,9,11],[1,3,6],[1,4,6],[1,5,9],[1,8,11],[2,3,8],[1,2,9],[3,4,7],[5,7,9],[2,8,10],[2,10,11],[1,7,10],[0,4,8],[0,1,6],[4,5,9],[5,6,10],[3,10,11],[8,9,11],[5,6,10],[0,7,10],[2,3,10],[0,8,9],[4,6,11],[1,9,11],[5,7,10],[2,8,9],[1,2,7],[1,5,9],[1,2,8],[5,7,11],[5,8,11],[0,9,11],[3,4,10],[2,3,10],[1,3,6],[3,4,9],[1,6,7],[3,7,10],[1,4,5],[2,3,6],[1,7,8],[1,5,10],[3,5,7],[3,7,8],[0,1,5],[2,6,11],[2,5,7],[0,3,9],[4,8,10],[1,2,6],[6,10,11],[1,7,8],[2,5,7],[3,5,11],[3,4,10],[0,3,4],[0,3,5],[5,8,10],[0,2,7],[7,9,11],[6,8,10],[6,7,10],[3,10,11],[4,8,9],[2,3,8],[3,5,6],[5,8,9],[4,9,11],[2,3,9],[3,4,11],[2,10,11],[2,4,7],[2,5,6],[2,5,10],[3,4,5],[6,10,11],[0,3,6],[1,3,5],[7,10,11],[3,4,5],[3,9,11],[5,9,10],[2,9,10],[0,1,5],[7,8,11],[5,6,10],[0,1,10],[2,3,11],[1,9,11],[1,2,5],[5,6,11],[0,2,3],[5,9,10]],[[0,3,6],[0,8,10],[4,5,7],[3,8,10],[0,1,5],[2,9,10],[4,5,6],[0,3,10],[3,8,10],[1,3,4],[2,5,9],[0,6,11],[1,5,7],[3,7,8],[0,6,7],[0,3,8],[4,6,11],[4,6,7],[2,4,10],[0,7,8],[1,8,9],[0,3,5],[2,4,9],[0,6,8],[1,4,11],[0,3,8],[0,9,11],[2,3,11],[0,4,5],[1,4,8],[1,2,10],[0,6,10],[0,4,11],[4,5,8],[1,3,7],[4,5,9],[0,4,11],[7,9,11],[1,4,10],[3,5,10],[1,2,10],[1,3,8],[2,4,8],[6,8,10],[0,9,10],[6,8,11],[3,5,9],[1,7,8],[6,7,9],[3,5,11],[7,8,11],[2,3,7],[2,3,11],[4,7,10],[4,7,9],[4,9,11],[2,6,10],[1,2,6],[3,6,8],[5,6,11],[1,7,10],[4,5,7],[0,2,8],[1,6,9],[1,2,5],[5,7,8],[0,5,11],[5,9,10],[2,7,10],[2,6,10],[0,6,8],[4,7,9],[2,5,9],[1,5,7],[3,7,10],[0,2,10],[3,6,8],[1,4,6],[6,9,10],[7,8,11],[0,2,6],[4,7,11],[1,3,7],[0,4,7],[1,5,9],[2,8,9],[1,4,11],[0,1,10],[8,10,11],[1,9,11],[2,3,4],[4,9,10],[3,5,6],[3,6,11],[0,2,9],[2,4,9],[8,10,11],[6,10,11],[0,1,11],[3,10,11],[3,7,9],[0,1,4],[0,3,8],[2,9,11],[4,8,10],[2,5,9],[1,5,8],[8,9,11],[1,7,9],[4,5,11],[9,10,11],[2,5,9],[3,5,8],[0,4,11],[0,6,11],[4,8,10],[2,4,11],[1,4,5],[2,8,10],[4,8,9],[0,2,10],[0,6,9],[0,5,9],[0,1,10],[0,5,9],[3,4,8],[3,4,7],[4,5,7],[0,3,6],[1,7,10],[0,6,9],[3,8,10],[5,6,8],[3,5,11],[1,3,11],[0,7,10],[3,7,9],[4,9,10],[2,9,10],[2,3,11],[7,9,11],[0,2,4],[3,6,10],[0,1,6],[0,1,7],[1,2,5],[1,2,3],[6,7,8],[2,3,5],[3,4,7],[1,3,10],[1,7,8],[0,2,5],[7,9,10],[3,6,7],[3,7,9],[0,2,6],[3,5,11],[1,2,7],[0,3,11],[5,6,10],[4,5,9],[0,2,9],[0,6,10],[1,6,8],[1,2,8],[0,6,8],[0,1,8],[1,3,8],[0,6,10],[1,4,8],[2,8,9],[0,5,9],[1,3,9],[1,2,11],[1,5,7],[2,4,8],[3,6,11],[2,3,6],[0,1,4],[1,6,8],[5,9,11],[0,2,6],[1,6,7],[2,7,11],[2,7,11],[6,10,11],[0,1,5],[2,3,9],[8,9,11],[0,7,8],[0,1,2],[3,5,8],[1,8,11],[6,7,9],[7,10,11],[3,10,11],[2,5,8],[1,3,11],[4,6,11],[0,3,9],[5,9,10],[1,2,6],[1,4,7],[6,7,11],[0,3,4],[0,3,8],[0,2,7],[0,3,11],[3,5,9],[0,10,11],[2,4,10],[0,3,4],[4,7,9],[0,7,8],[8,10,11],[2,6,10],[5,6,9],[0,1,6],[1,2,3],[2,5,7],[5,6,9],[8,10,11],[5,8,9],[2,3,11],[1,2,4],[1,4,10],[1,2,7],[7,8,10],[1,6,8],[1,3,11],[2,3,10],[0,7,8],[8,10,11],[5,6,8],[3,7,8],[9,10,11],[0,1,5],[0,5,6],[2,7,9],[0,2,9],[0,1,7],[0,1,10],[0,4,11],[0,4,6],[0,2,11],[3,5,7],[5,7,11],[1,4,8],[2,4,6],[4,6,9],[1,4,8],[0,1,10],[3,8,10],[0,3,7],[5,10,11],[4,9,10],[0,5,9],[2,7,10],[1,2,6],[2,5,8],[9,10,11],[0,4,9],[4,5,11],[4,6,8],[1,8,10],[2,4,9],[1,2,5],[1,2,10],[0,1,3],[0,4,11],[0,4,6],[3,5,7],[4,8,10],[3,8,10],[2,8,10],[0,2,3],[5,9,10],[5,10,11],[2,9,11],[0,3,8],[2,4,7],[1,3,7],[6,7,8],[6,8,11],[1,5,8],[1,4,7],[3,6,7],[6,7,9],[7,9,11],[1,4,9],[2,10,11],[5,7,11],[2,6,9],[0,8,11],[7,8,9],[0,1,8],[3,6,7],[5,7,8],[0,6,11],[0,4,7],[0,3,11],[7,9,11],[2,7,10],[1,2,8],[1,3,10],[1,3,8],[0,4,7],[3,4,6],[3,7,8],[8,9,10],[0,4,11],[1,2,4],[3,5,7],[3,10,11],[1,5,7],[1,8,9],[1,6,8],[4,6,8],[8,10,11],[1,3,7],[4,5,11],[0,3,5],[2,3,5],[0,5,8],[4,5,6],[2,8,10],[4,6,8],[4,5,10],[0,7,11],[1,7,11],[1,3,8],[5,6,9],[4,9,10],[0,4,11],[7,10,11],[0,4,6],[0,3,8],[2,3,9],[0,2,4],[1,5,11],[0,5,7],[2,3,6],[8,10,11],[1,4,10],[0,3,10],[2,7,11],[4,8,9],[4,6,8],[1,2,7],[1,7,11],[6,7,9],[3,8,10],[3,6,8],[2,4,7],[3,6,9],[3,4,10],[0,8,10],[8,9,10],[4,8,11],[0,7,11],[2,5,11],[6,8,9],[4,6,11],[4,9,11],[1,4,11],[3,5,11],[5,9,11],[2,6,11],[1,8,11],[1,2,5],[2,4,8],[4,8,11],[1,6,11],[1,4,11],[1,4,5],[0,1,9],[2,4,11],[2,5,10],[2,3,10],[1,4,7],[5,7,11],[0,6,11],[0,2,3],[0,4,6],[0,4,5],[1,3,4],[0,6,8],[0,1,4],[1,6,7],[0,6,7],[3,4,11],[7,8,9],[6,7,11],[1,2,4],[1,4,5],[0,8,11],[4,6,10],[1,7,10],[4,8,11],[1,3,5],[2,8,9],[5,9,11],[6,10,11],[0,1,3],[3,5,8],[2,5,6],[6,9,11],[3,4,5],[5,8,10],[4,8,10],[6,8,9],[0,3,9],[0,6,8],[0,3,7],[0,9,11],[5,9,10],[1,2,9],[2,3,8],[4,7,8],[5,10,11],[0,6,8],[5,7,8],[6,7,8],[0,7,8],[0,4,5],[1,7,8],[1,5,8],[0,5,10],[0,7,9],[1,6,7],[0,3,7],[1,2,6],[2,3,11],[2,5,8],[1,5,9],[4,8,11],[4,8,9],[0,7,11],[5,8,10],[1,6,11],[3,4,9],[0,2,7],[3,5,9],[0,5,6],[3,7,9],[3,8,10],[5,9,10],[2,8,9],[0,2,5],[1,2,4],[2,4,6],[2,4,5],[1,2,10],[2,3,10],[5,8,10],[4,7,10],[4,7,8],[2,5,6],[8,9,10],[1,5,9],[6,8,9],[4,8,10],[0,3,6],[3,7,10],[4,7,10],[0,10,11],[0,4,7],[1,10,11],[2,3,8],[6,8,10],[2,10,11],[0,1,4],[0,3,11],[2,5,8],[6,9,10],[3,4,10],[1,9,11],[8,9,11],[0,9,10],[2,4,8],[1,7,8],[6,7,11],[0,1,9],[1,9,11],[2,4,9],[4,9,10],[3,4,11],[0,4,7],[2,9,10],[3,8,9],[1,5,11],[1,2,8],[0,1,4],[0,6,8],[5,7,9],[0,3,9],[2,5,7],[5,7,11],[6,8,11],[7,8,11],[4,7,8],[2,5,7],[6,9,11],[3,6,9],[2,6,8],[1,6,7],[4,9,10],[3,8,10],[0,5,11],[2,3,7],[3,5,7]],[[2,6,9],[4,8,10],[7,10,11],[3,5,7],[7,8,11],[0,4,9],[1,4,11],[0,7,9],[0,4,10],[0,8,9],[4,5,7],[1,6,11],[3,7,8],[2,5,10],[6,10,11],[2,8,9],[2,8,9],[1,5,11],[4,5,11],[5,9,10],[0,1,9],[0,9,10],[2,4,5],[0,8,11],[0,7,11],[5,9,11],[0,4,11],[2,3,8],[3,5,10],[3,4,8],[2,4,8],[0,5,9],[2,9,10],[2,5,9],[5,8,10],[7,8,10],[5,7,9],[0,3,9],[3,4,8],[0,4,7],[4,8,10],[3,4,11],[0,6,7],[8,9,11],[1,5,7],[0,3,7],[3,5,7],[2,6,9],[4,5,11],[1,3,5],[0,3,5],[9,10,11],[3,6,10],[5,7,9],[1,4,10],[1,5,9],[4,6,9],[1,3,9],[2,4,9],[8,9,10],[0,4,9],[0,1,4],[3,9,11],[8,9,11],[1,4,8],[3,9,10],[0,4,10],[1,7,10],[2,5,10],[4,6,9],[2,8,10],[4,6,11],[9,10,11],[4,7,11],[3,5,7],[1,7,8],[0,2,11],[5,7,8],[6,9,10],[2,7,8],[8,9,10],[1,5,7],[0,4,10],[6,7,8],[1,7,9],[6,8,9],[5,7,8],[1,7,8],[3,5,6],[0,6,8],[3,8,11],[2,4,6],[2,4,6],[1,6,8],[4,6,10],[2,4,5],[2,5,8],[0,1,5],[3,4,9],[2,4,9],[6,9,10],[5,6,9],[1,3,10],[2,4,8],[5,6,9],[2,7,10],[0,2,9],[0,5,7],[3,4,11],[4,8,9],[3,5,8],[2,3,9],[2,4,9],[2,4,5],[0,7,8],[2,5,11],[3,6,9],[1,4,8],[0,6,11],[0,4,5],[0,2,10],[0,1,7],[6,7,11],[1,8,11],[5,7,10],[0,8,10],[4,5,10],[5,7,9],[2,4,6],[2,6,7],[1,3,7],[2,7,10],[2,5,11],[3,4,6],[1,7,8],[6,7,9],[0,6,7],[5,6,8],[2,9,10],[3,7,11],[6,8,10],[4,5,11],[0,1,9],[2,6,11],[5,8,9],[0,2,8],[7,8,11],[5,7,11],[5,8,11],[8,10,11],[0,6,8],[2,6,10],[0,8,9],[2,3,8],[0,3,11],[8,10,11],[0,1,9],[6,8,10],[4,6,10],[7,8,11],[3,9,10],[2,10,11],[0,1,7],[5,8,10],[4,6,10],[1,8,11],[0,5,8],[1,4,10],[6,9,11],[1,9,11],[0,9,10],[6,8,10],[0,8,9],[3,6,8],[4,6,7],[0,6,9],[4,5,6],[0,1,10],[1,2,9],[1,9,11],[3,5,9],[5,6,10],[1,6,9],[7,8,11],[5,8,9],[0,6,11],[1,9,10],[4,5,10],[0,2,9],[1,2,9],[3,4,10],[0,10,11],[3,7,10],[2,9,11],[5,9,10],[2,3,6],[3,4,6],[1,2,7],[0,9,11],[2,6,11],[4,9,10],[0,1,3],[6,7,11],[2,6,10],[1,3,10],[5,6,9],[0,5,8],[2,6,11],[1,5,8],[1,3,7],[1,7,11],[2,4,11],[0,5,9],[2,3,9],[9,10,11],[2,6,9],[2,5,9],[0,5,8],[0,8,10],[3,4,8],[6,8,10],[0,1,10],[1,6,7],[1,9,10],[0,1,11],[1,7,10],[7,9,10],[0,4,8],[6,7,9],[0,5,10],[2,3,4],[1,8,10],[4,8,10],[1,3,6],[2,5,7],[4,8,9],[5,10,11],[0,2,7],[4,5,8],[4,5,9],[4,8,9],[2,3,6],[1,7,10],[1,3,10],[5,7,10],[8,9,10],[2,5,11],[4,8,10],[0,4,5],[1,6,8],[0,9,11],[1,2,11],[1,6,10],[7,8,9],[5,9,11],[3,6,11],[3,10,11],[5,6,10],[0,4,5],[1,5,6],[2,8,9],[2,10,11],[1,2,8],[3,7,9],[2,4,10],[1,2,7],[1,7,8],[0,3,7],[3,4,9],[2,3,11],[1,3,6],[1,2,11],[0,4,7],[5,8,10],[4,8,9],[0,2,11],[0,6,9],[7,8,9],[3,6,8],[3,9,11],[3,9,10],[3,4,8],[8,9,11],[1,5,8],[3,7,9],[3,6,10],[0,1,8],[1,5,6],[0,3,9],[1,4,5],[0,2,3],[0,8,11],[0,4,10],[2,7,9],[7,9,11],[2,3,6],[6,7,8],[3,9,11],[5,6,8],[5,8,11],[3,8,10],[2,6,7],[0,8,9],[0,3,11],[2,4,10],[0,3,11],[1,2,6],[3,5,6],[0,1,2],[0,3,10],[1,4,10],[5,8,11],[0,7,10],[3,8,11],[0,4,11],[2,4,7],[0,1,8],[1,4,6],[4,8,10],[1,3,6],[0,6,8],[3,4,6],[0,4,5],[2,3,7],[3,6,7],[7,10,11],[2,8,11],[6,7,9],[2,8,9],[7,8,10],[3,9,11],[1,2,11],[1,4,9],[5,9,10],[0,6,7],[2,4,9],[0,6,10],[3,4,7],[3,4,6],[0,6,11],[2,6,7],[4,8,11],[1,5,11],[1,3,6],[5,6,9],[1,6,7],[0,2,8],[6,10,11],[1,3,10],[2,9,11],[2,8,11],[1,2,6],[3,4,5],[0,5,9],[3,7,8],[5,6,11],[4,5,8],[2,8,9],[4,6,9],[2,5,9],[3,5,11],[2,5,10],[1,3,5],[5,8,10],[1,3,5],[5,7,8],[5,6,10],[1,2,4],[2,7,10],[0,3,4],[1,2,6],[7,9,10],[2,5,7],[0,4,7],[1,5,10],[0,1,5],[7,9,10],[1,2,6],[3,4,6],[2,5,9],[2,3,8],[3,5,8],[7,8,9],[0,6,7],[0,8,9],[0,2,11],[0,7,8],[1,8,9],[3,6,11],[0,6,9],[0,1,4],[3,4,5],[0,8,9],[1,9,10],[2,6,10],[0,3,5],[0,4,5],[5,10,11],[2,5,10],[1,2,11],[5,6,8],[0,4,9],[3,6,10],[1,9,11],[4,7,11],[2,5,8],[1,8,9],[4,8,11],[2,4,5],[3,6,9],[0,2,7],[4,6,11],[0,8,10],[7,8,9],[0,5,6],[0,2,5],[3,6,8],[3,6,11],[2,7,8],[2,5,9],[2,4,10],[1,9,11],[1,6,8],[1,5,10],[0,2,7],[7,8,11],[0,6,11],[4,9,10],[1,2,11],[4,6,11],[0,2,4],[1,5,9],[0,4,9],[0,3,6],[2,7,8],[2,5,10],[4,5,9],[6,9,10],[2,7,8],[5,7,8],[5,7,8],[1,7,11],[3,4,11],[0,5,11],[7,8,11],[0,2,6],[1,5,11],[3,9,11],[0,5,10],[8,9,11],[2,10,11],[1,9,11],[0,3,10],[1,3,7],[4,9,11],[1,2,3],[2,7,10],[5,7,9],[1,2,9],[5,8,9],[1,6,10],[1,7,10],[0,4,5],[2,4,7],[1,6,9],[0,5,8],[5,6,7],[1,4,7],[5,9,11],[1,5,9],[1,9,11],[1,4,6],[4,5,11],[1,6,11],[0,2,6],[7,8,10],[2,3,7],[5,6,7],[4,5,8],[8,10,11],[2,9,11],[2,3,10],[1,5,9],[7,8,10],[0,2,6],[0,4,9],[1,4,5],[2,4,7],[0,3,6],[1,8,9],[3,5,10],[1,2,3],[1,4,7],[1,3,6],[4,7,10],[1,2,10],[5,8,9],[7,8,11],[6,8,10],[1,2,11],[7,9,11],[1,7,11],[2,4,11],[0,1,10],[2,6,11],[6,9,10],[0,5,8],[0,1,5],[1,4,7],[0,6,7],[0,2,4],[3,4,11]],[[0,2,8],[1,3,10],[0,6,11],[1,7,9],[5,8,9],[0,1,9],[3,7,11],[0,1,2],[3,7,9],[1,2,4],[3,7,8],[2,6,7],[1,6,10],[3,4,10],[2,6,10],[2,5,8],[2,3,5],[1,5,11],[1,7,11],[3,4,9],[2,4,5],[1,2,4],[4,8,10],[3,5,11],[0,6,9],[0,2,3],[1,5,9],[0,5,8],[0,1,7],[3,5,10],[2,4,10],[2,8,10],[0,1,3],[1,3,9],[2,3,9],[3,5,6],[0,2,3],[0,4,8],[2,8,10],[2,6,8],[4,6,10],[2,4,10],[2,6,11],[0,4,7],[2,5,9],[4,10,11],[2,3,9],[1,4,5],[2,3,5],[1,3,5],[7,9,11],[0,3,6],[2,6,11],[0,7,8],[2,3,10],[5,6,7],[0,8,10],[1,8,11],[3,5,11],[1,3,10],[1,7,11],[5,6,7],[0,1,8],[0,4,10],[0,5,6],[0,1,3],[3,8,9],[0,1,2],[1,3,10],[0,8,10],[0,3,6],[6,7,9],[1,2,4],[4,8,9],[0,1,6],[0,1,2],[4,5,8],[2,5,8],[0,2,8],[4,6,10],[0,8,10],[0,5,10],[0,4,8],[1,2,11],[0,1,7],[1,6,10],[8,10,11],[6,8,10],[2,4,8],[2,3,9],[8,9,11],[5,8,9],[5,7,10],[1,3,10],[1,5,6],[2,4,8],[1,3,10],[3,9,11],[0,3,4],[4,5,8],[0,1,8],[0,1,2],[1,8,11],[3,6,7],[3,4,5],[0,5,11],[1,3,9],[1,2,5],[2,4,6],[1,4,9],[4,6,10],[5,6,11],[4,6,9],[7,8,11],[1,4,10],[2,8,11],[2,4,5],[3,7,9],[0,4,8],[3,6,7],[2,3,11],[1,6,11],[2,4,8],[3,4,11],[4,7,9],[1,6,10],[1,7,9],[0,3,9],[2,8,9],[1,4,7],[3,6,11],[0,7,10],[3,4,10],[1,2,5],[0,4,8],[1,2,6],[0,3,10],[0,4,8],[2,7,8],[1,5,10],[0,4,9],[4,5,10],[3,4,6],[1,4,10],[1,2,11],[2,5,7],[0,8,9],[8,9,10],[0,6,7],[6,7,10],[0,2,5],[0,1,3],[1,4,9],[1,2,10],[1,2,4],[0,5,11],[0,1,5],[0,2,6],[4,5,11],[2,4,7],[3,6,8],[3,6,10],[5,8,9],[1,4,5],[2,5,10],[0,3,8],[8,10,11],[7,8,9],[3,5,9],[0,1,10],[0,9,11],[1,4,7],[0,7,8],[5,7,9],[3,5,11],[1,2,7],[2,7,10],[0,2,4],[1,3,5],[2,4,10],[2,5,11],[3,5,9],[4,8,11],[8,10,11],[0,10,11],[4,7,8],[2,8,9],[0,5,7],[3,8,9],[5,6,11],[2,4,9],[1,2,10],[0,6,7],[1,7,10],[0,6,10],[2,7,9],[4,8,11],[2,3,8],[0,10,11],[1,2,8],[1,6,8],[0,4,8],[1,3,8],[3,5,6],[0,9,11],[1,5,7],[1,3,11],[4,5,11],[2,6,9],[5,6,7],[2,3,6],[6,7,9],[1,6,11],[2,3,7],[2,3,8],[0,5,8],[4,8,11],[6,8,11],[5,6,8],[4,6,11],[2,5,6],[1,4,5],[1,2,6],[2,10,11],[1,4,8],[1,2,11],[6,8,9],[2,4,10],[0,4,9],[6,7,8],[3,6,9],[9,10,11],[3,4,11],[5,9,10],[4,6,7],[1,9,10],[2,5,8],[1,4,5],[0,7,11],[3,4,9],[5,6,9],[0,10,11],[0,3,11],[4,6,11],[0,1,11],[0,2,3],[0,2,4],[5,10,11],[4,6,9],[2,6,10],[7,10,11],[6,7,11],[2,6,7],[6,7,8],[5,6,11],[1,2,6],[4,8,11],[1,4,11],[1,5,7],[0,5,8],[2,6,8],[0,5,8],[6,9,10],[7,10,11],[8,10,11],[5,9,10],[4,7,11],[3,4,10],[1,7,10],[4,10,11],[3,7,11],[2,7,8],[0,6,11],[1,3,4],[4,8,10],[5,6,9],[0,2,10],[1,6,9],[7,8,11],[2,3,6],[0,2,8],[0,6,11],[2,6,10],[0,4,7],[0,8,10],[3,7,9],[4,5,11],[6,8,11],[3,5,8],[2,3,11],[0,1,7],[7,9,10],[0,5,11],[6,7,10],[1,8,9],[2,8,10],[3,5,10],[2,7,10],[2,3,5],[1,2,8],[0,3,9],[5,6,11],[1,4,6],[4,6,7],[2,6,8],[0,5,9],[7,10,11],[3,9,11],[0,4,9],[0,4,5],[4,7,8],[1,2,5],[6,9,11],[3,5,8],[0,7,11],[1,8,9],[4,5,8],[2,9,10],[0,1,3],[0,2,8],[2,4,6],[4,6,11],[1,4,5],[8,10,11],[1,7,8],[0,2,10],[1,4,10],[0,1,3],[0,1,5],[0,3,7],[5,7,10],[1,4,5],[2,3,4],[0,10,11],[4,6,7],[0,8,10],[0,3,9],[2,5,6],[0,6,11],[5,9,10],[6,8,10],[7,9,10],[0,2,8],[2,4,11],[6,8,10],[0,1,7],[3,9,10],[3,5,11],[1,4,6],[6,7,11],[1,6,11],[1,3,10],[5,9,11],[5,6,11],[0,3,7],[0,6,10],[4,9,10],[1,5,8],[1,2,6],[0,3,11],[1,5,10],[3,9,10],[6,10,11],[2,10,11],[4,8,10],[3,5,7],[1,6,7],[1,10,11],[3,4,11],[2,3,7],[1,2,11],[0,2,11],[1,4,8],[3,6,8],[1,8,9],[2,7,10],[1,2,10],[0,9,11],[1,10,11],[6,7,9],[3,5,9],[3,5,10],[0,2,7],[4,10,11],[0,7,11],[0,4,10],[4,8,10],[8,9,10],[0,6,9],[2,9,10],[2,4,7],[1,2,8],[2,9,11],[3,4,11],[1,3,7],[2,4,8],[7,10,11],[4,10,11],[0,5,11],[0,1,7],[3,6,8],[3,4,8],[4,7,11],[2,5,11],[3,4,5],[2,3,8],[3,6,8],[2,3,11],[7,10,11],[1,3,9],[0,5,7],[4,8,11],[0,8,11],[4,9,10],[8,10,11],[3,7,8],[1,2,4],[0,1,7],[1,2,10],[4,5,9],[9,10,11],[6,8,10],[1,2,3],[2,3,8],[1,6,9],[0,7,9],[9,10,11],[1,7,9],[2,6,7],[1,2,8],[7,8,9],[3,4,10],[3,4,9],[2,6,7],[1,3,11],[1,3,5],[3,7,8],[0,2,3],[0,8,11],[2,4,11],[5,9,11],[6,7,9],[0,6,9],[3,8,11],[1,7,10],[7,8,9],[3,6,8],[2,7,10],[0,3,10],[1,5,10],[0,5,10],[3,4,5],[0,3,7],[1,2,7],[3,5,11],[2,9,10],[0,3,10],[1,3,4],[6,8,11],[1,10,11],[2,4,10],[7,10,11],[0,8,9],[6,7,11],[1,5,8],[0,1,3],[1,2,8],[0,9,10],[1,4,6],[2,4,7],[5,6,9],[7,10,11],[2,6,7],[1,5,9],[1,9,11],[1,7,9],[4,9,10],[4,10,11],[2,5,6],[3,6,7],[2,6,8],[4,8,10],[0,5,11],[0,1,7],[2,6,8],[0,6,8],[0,5,6],[1,7,9],[0,7,9],[3,6,10],[5,7,9],[0,7,8],[1,4,8],[4,6,9],[2,5,6],[0,6,10],[5,6,11],[6,7,9],[3,6,10],[3,5,9],[3,7,9],[0,3,5],[5,6,10],[1,8,11],[1,2,3],[0,6,9],[2,4,6],[2,9,11],[2,6,7],[0,4,6],[1,5,8],[1,2,7]],[[2,7,10],[2,5,7],[2,3,10],[4,5,10],[6,8,11],[2,3,9],[3,4,10],[1,7,8],[2,4,11],[7,8,9],[0,5,8],[0,3,5],[0,7,8],[4,6,11],[1,3,8],[5,6,11],[0,6,9],[4,7,8],[2,4,11],[8,9,10],[1,7,11],[3,5,11],[8,9,11],[2,4,8],[0,8,10],[5,7,8],[1,2,7],[2,5,6],[1,5,9],[7,8,11],[0,4,10],[5,6,8],[0,3,11],[2,8,11],[2,3,9],[0,6,8],[2,5,7],[0,4,11],[2,7,9],[5,9,10],[1,4,7],[3,9,10],[9,10,11],[0,3,10],[6,9,11],[0,1,5],[2,3,5],[4,5,7],[2,6,10],[3,5,10],[4,7,11],[1,2,7],[6,7,10],[1,2,8],[6,8,11],[0,4,11],[2,7,8],[4,9,10],[1,6,11],[0,4,8],[2,6,9],[4,9,11],[0,1,6],[3,7,11],[4,8,11],[0,10,11],[0,4,8],[3,5,8],[0,5,8],[0,4,6],[1,10,11],[7,9,11],[0,5,8],[1,4,9],[4,6,8],[1,5,7],[4,5,10],[0,1,5],[4,7,9],[4,9,11],[4,5,11],[7,8,11],[3,6,9],[4,10,11],[2,5,8],[3,6,7],[2,3,8],[1,7,10],[3,6,8],[4,5,9],[7,8,11],[0,1,11],[2,6,9],[2,3,4],[5,6,11],[0,6,11],[6,9,10],[0,4,8],[3,5,7],[3,4,5],[0,1,6],[2,4,9],[3,5,11],[3,6,11],[3,6,11],[6,10,11],[6,7,8],[4,7,8],[2,4,9],[1,3,10],[4,5,10],[1,5,7],[7,8,9],[5,6,8],[1,2,10],[6,7,8],[5,6,11],[2,8,10],[3,5,8],[2,5,9],[0,4,9],[3,7,9],[2,8,9],[0,7,10],[0,4,9],[0,2,5],[2,8,10],[5,8,9],[4,9,10],[0,3,9],[5,8,9],[1,2,8],[1,2,6],[0,3,8],[4,5,10],[1,9,11],[3,7,10],[1,5,8],[0,4,8],[5,7,11],[4,5,6],[3,7,11],[3,4,10],[3,7,9],[1,3,6],[3,4,5],[2,3,7],[5,10,11],[5,9,11],[1,6,7],[0,6,8],[2,6,11],[1,5,10],[1,3,10],[2,8,10],[5,6,10],[3,4,7],[5,9,11],[1,2,3],[1,3,11],[4,5,10],[2,3,7],[1,2,11],[0,4,11],[0,4,7],[1,4,8],[2,9,10],[0,1,3],[0,3,11],[7,8,11],[0,3,6],[0,4,6],[0,6,9],[1,4,7],[1,7,11],[4,5,6],[6,9,11],[2,6,8],[3,8,10],[2,5,10],[3,5,11],[3,4,8],[0,3,11],[4,5,8],[4,6,11],[4,5,11],[1,2,10],[0,7,8],[1,3,9],[1,7,9],[4,7,11],[3,7,8],[2,4,10],[3,4,6],[2,4,7],[0,8,9],[1,3,9],[7,8,11],[0,2,10],[2,6,7],[0,4,10],[4,8,11],[6,8,11],[1,5,10],[4,5,7],[2,3,8],[0,7,8],[4,10,11],[3,7,9],[6,7,10],[2,3,7],[2,4,7],[1,9,11],[3,6,9],[6,10,11],[0,8,10],[1,6,10],[1,4,5],[5,9,10],[0,3,6],[9,10,11],[5,6,8],[6,9,10],[5,7,8],[0,5,6],[3,8,10],[3,5,9],[3,8,10],[3,7,9],[3,8,9],[1,4,5],[0,5,6],[0,6,9],[2,4,11],[1,3,9],[4,8,9],[4,7,10],[0,3,5],[3,4,6],[0,7,8],[1,5,9],[6,8,10],[4,5,8],[2,8,10],[1,4,8],[2,9,11],[2,3,10],[0,1,7],[2,6,8],[2,3,4],[0,5,10],[1,2,3],[4,10,11],[6,7,9],[0,5,8],[1,7,11],[4,6,8],[2,5,8],[3,4,7],[0,7,8],[8,10,11],[4,7,11],[2,3,7],[2,4,6],[3,4,7],[0,4,10],[2,10,11],[1,2,4],[0,3,7],[4,5,6],[5,6,10],[3,6,8],[3,7,10],[1,4,9],[0,2,3],[1,8,11],[3,6,11],[3,7,10],[2,7,11],[1,7,11],[6,7,10],[3,4,7],[0,1,9],[2,5,9],[3,6,8],[1,9,11],[0,7,11],[1,2,9],[0,8,10],[4,6,11],[0,7,9],[1,6,7],[1,4,6],[0,3,8],[1,4,11],[0,1,3],[3,4,10],[1,7,11],[0,2,7],[4,10,11],[3,8,9],[0,8,10],[5,6,7],[0,10,11],[1,3,8],[0,6,7],[0,9,10],[3,6,11],[1,3,10],[1,2,4],[0,2,5],[0,5,6],[3,10,11],[7,9,10],[0,3,4],[4,7,11],[0,5,8],[2,8,9],[8,10,11],[1,6,11],[6,8,10],[6,7,11],[0,8,11],[9,10,11],[1,7,11],[6,7,8],[1,3,10],[3,4,7],[4,10,11],[0,1,7],[0,1,3],[3,6,9],[1,4,5],[0,5,10],[4,9,11],[0,1,8],[2,5,11],[0,1,8],[3,5,7],[2,4,6],[1,4,8],[0,3,11],[1,6,10],[0,5,10],[7,8,9],[0,8,11],[2,10,11],[3,8,11],[6,7,9],[3,10,11],[2,4,11],[7,8,9],[3,6,11],[2,4,8],[4,10,11],[5,6,7],[1,8,9],[2,5,9],[4,5,9],[1,2,11],[0,8,9],[0,4,7],[1,3,8],[3,7,8],[8,9,11],[1,2,3],[0,1,9],[0,5,9],[1,4,11],[2,5,7],[0,6,9],[2,4,8],[2,6,11],[0,1,9],[0,4,9],[1,6,7],[1,8,10],[1,6,9],[0,3,10],[0,4,5],[0,4,6],[2,5,11],[7,8,11],[3,7,11],[0,6,7],[2,3,4],[0,1,8],[0,3,8],[1,5,7],[1,6,10],[0,1,8],[0,3,5],[0,1,4],[3,4,7],[4,5,6],[2,7,11],[5,7,8],[0,2,8],[3,5,6],[0,1,11],[4,6,10],[0,2,6],[0,8,11],[1,4,5],[1,4,7],[0,6,8],[0,1,11],[9,10,11],[2,4,5],[1,6,7],[4,7,9],[7,8,10],[1,4,7],[1,2,10],[1,8,9],[2,5,11],[3,10,11],[2,5,8],[2,3,4],[0,5,10],[0,2,9],[1,3,9],[2,3,10],[1,5,6],[0,1,6],[1,5,11],[0,6,7],[4,9,11],[2,6,8],[3,10,11],[1,2,4],[5,6,9],[5,7,10],[2,7,8],[1,5,9],[0,6,10],[0,4,9],[2,10,11],[5,9,10],[4,6,11],[3,7,9],[2,4,5],[1,7,8],[0,5,9],[4,5,8],[0,7,8],[4,6,8],[3,6,11],[1,2,4],[6,9,10],[2,3,11],[5,7,10],[4,9,11],[1,2,10],[4,9,10],[2,8,10],[3,7,9],[2,3,5],[7,9,11],[2,3,7],[0,2,10],[0,9,10],[0,2,8],[5,8,10],[3,6,11],[2,9,10],[2,9,10],[5,6,11],[0,1,7],[0,2,10],[0,9,11],[0,3,5],[2,3,10],[3,5,7],[0,1,5],[1,8,9],[3,6,7],[0,6,11],[8,9,11],[2,5,10],[3,6,9],[1,2,8],[4,6,8],[0,5,9],[6,7,10],[1,6,9],[5,6,8],[0,2,10],[0,3,5],[2,6,7],[5,7,8],[6,8,10],[2,5,8],[4,5,9],[3,6,8],[0,2,9],[0,1,11],[3,5,11],[2,10,11],[3,7,10],[9,10,11],[1,5,10],[6,8,11],[2,3,11],[0,1,9],[1,3,8],[0,5,9],[2,3,4],[1,4,11],[0,8,10],[0,6,10],[2,5,7]],[[1,5,6],[1,7,11],[3,9,11],[0,7,8],[2,4,5],[1,7,8],[4,9,10],[3,4,9],[3,5,7],[2,5,7],[1,3,9],[3,7,8],[1,5,9],[3,5,6],[6,8,9],[3,7,8],[1,6,8],[3,9,11],[0,1,7],[1,7,10],[1,4,11],[0,6,8],[1,3,8],[2,7,11],[6,9,10],[2,5,7],[0,1,3],[3,9,10],[0,3,11],[0,7,8],[5,7,8],[0,4,8],[4,8,10],[4,6,10],[1,5,10],[3,6,7],[1,2,3],[1,3,11],[2,6,10],[2,6,7],[7,9,10],[1,9,11],[0,4,7],[2,5,8],[0,2,4],[0,4,8],[0,4,6],[3,8,9],[5,9,10],[1,8,10],[1,2,10],[3,7,11],[0,4,9],[0,2,11],[0,2,3],[1,9,11],[0,2,8],[3,6,11],[0,2,6],[2,3,9],[0,9,11],[1,4,10],[4,7,11],[4,9,11],[0,3,9],[3,6,10],[0,1,5],[3,10,11],[4,8,9],[0,2,6],[5,6,9],[1,4,7],[1,4,8],[0,5,10],[4,5,10],[3,9,10],[0,1,2],[1,2,11],[4,9,10],[1,7,9],[1,4,10],[5,6,8],[0,3,6],[8,9,10],[5,9,11],[0,2,9],[5,8,9],[1,3,4],[2,4,8],[6,7,11],[0,1,3],[8,9,10],[1,3,8],[4,5,10],[2,4,5],[7,8,10],[2,7,8],[2,7,11],[2,4,7],[1,3,6],[5,6,10],[1,6,11],[8,10,11],[0,1,5],[5,7,11],[1,7,10],[4,5,6],[3,8,10],[2,5,10],[0,4,11],[2,6,10],[0,4,5],[0,2,6],[0,2,5],[4,6,10],[2,3,4],[1,9,11],[0,6,9],[0,6,10],[3,7,8],[3,6,11],[5,6,8],[1,6,10],[6,7,8],[1,2,5],[6,8,10],[7,9,11],[1,6,9],[0,2,5],[2,4,7],[5,8,9],[3,5,8],[6,7,10],[3,5,11],[0,5,9],[1,4,11],[2,3,8],[3,7,9],[1,3,6],[0,1,9],[1,5,8],[5,8,11],[6,8,9],[0,6,7],[2,8,10],[2,8,9],[6,7,10],[0,2,9],[0,5,11],[4,6,9],[0,1,3],[5,8,10],[1,2,5],[3,7,8],[4,7,9],[0,7,10],[0,8,10],[2,3,11],[1,3,5],[1,2,7],[1,3,6],[1,8,10],[1,2,10],[0,4,8],[3,5,9],[0,3,7],[0,5,6],[4,5,7],[0,1,6],[0,7,9],[2,4,5],[0,7,11],[4,6,9],[0,4,9],[3,6,10],[1,3,5],[2,5,11],[0,1,6],[1,8,11],[3,4,6],[3,5,8],[1,4,8],[0,4,5],[0,4,8],[3,4,10],[4,7,8],[0,1,10],[2,8,10],[1,8,9],[6,10,11],[1,5,10],[5,9,11],[1,2,7],[1,3,9],[0,4,8],[3,9,10],[5,7,10],[2,6,10],[3,6,9],[1,2,3],[4,5,8],[1,3,11],[4,7,11],[2,7,10],[7,9,10],[0,4,10],[1,3,9],[6,8,10],[1,7,9],[3,4,7],[1,5,8],[6,7,9],[1,4,7],[1,3,7],[2,8,10],[2,5,11],[0,7,10],[0,1,5],[6,8,9],[1,7,8],[3,6,9],[3,8,10],[0,2,4],[1,6,11],[3,4,7],[0,3,8],[0,2,7],[0,6,9],[0,7,8],[3,7,9],[3,4,11],[7,8,10],[3,4,11],[2,4,6],[3,7,9],[0,5,8],[0,4,7],[1,9,10],[3,5,9],[2,5,8],[3,4,7],[1,4,10],[0,1,2],[5,7,10],[1,6,9],[0,5,6],[1,8,9],[1,2,9],[1,4,8],[0,1,9],[0,4,10],[2,6,9],[0,2,3],[5,7,10],[2,8,9],[1,2,4],[0,2,11],[0,1,11],[1,5,11],[0,3,11],[6,8,9],[0,2,10],[2,3,11],[0,1,5],[7,8,11],[2,6,11],[7,10,11],[0,5,10],[0,4,6],[0,4,6],[4,6,7],[0,4,6],[6,7,9],[3,7,11],[3,5,11],[3,5,7],[1,7,10],[1,3,9],[2,7,8],[0,2,6],[0,6,11],[0,7,9],[0,5,9],[3,5,11],[0,4,6],[5,6,9],[3,4,11],[0,6,9],[3,5,8],[0,5,9],[0,9,11],[5,6,10],[4,6,10],[6,7,9],[0,6,9],[2,4,5],[0,7,10],[1,5,11],[3,4,7],[5,10,11],[0,4,9],[4,7,11],[4,7,9],[0,3,8],[0,2,9],[0,1,8],[1,10,11],[2,5,9],[3,5,10],[2,3,5],[5,6,7],[4,6,7],[1,3,6],[5,7,11],[3,7,10],[1,4,5],[2,4,10],[0,6,9],[6,7,8],[0,1,11],[2,5,9],[1,4,11],[3,6,7],[1,6,7],[2,4,9],[0,2,6],[1,8,11],[0,2,7],[5,8,9],[3,6,9],[0,4,11],[1,8,11],[4,5,6],[6,8,9],[0,3,5],[1,2,4],[4,9,11],[3,6,11],[5,6,9],[0,4,6],[2,9,10],[2,6,9],[1,5,8],[2,4,9],[5,7,8],[4,5,7],[5,7,10],[0,1,10],[2,3,10],[3,8,9],[3,4,11],[0,7,8],[2,10,11],[3,5,11],[0,2,11],[1,3,8],[0,4,5],[2,3,10],[4,9,11],[1,2,11],[8,9,11],[0,5,11],[1,7,9],[3,4,10],[4,5,10],[1,5,11],[5,7,9],[7,8,10],[1,3,8],[2,6,10],[4,6,7],[3,6,8],[4,6,10],[9,10,11],[3,5,9],[6,7,11],[1,4,7],[1,5,10],[6,8,10],[1,7,11],[4,7,8],[3,4,6],[2,8,11],[2,8,9],[5,6,10],[2,10,11],[6,9,11],[0,5,11],[0,4,8],[3,4,6],[6,9,11],[2,3,8],[1,2,4],[1,4,10],[1,7,10],[5,7,11],[3,6,11],[0,3,5],[8,10,11],[7,10,11],[0,7,10],[6,10,11],[1,4,10],[2,7,10],[2,3,4],[1,6,10],[1,3,10],[0,1,2],[3,4,5],[3,4,7],[4,10,11],[0,7,11],[3,4,7],[0,1,2],[0,2,5],[5,6,10],[3,7,11],[4,5,10],[5,7,11],[0,5,10],[0,4,8],[3,4,10],[0,5,8],[1,3,5],[1,3,7],[7,8,10],[2,9,11],[0,5,7],[0,3,8],[5,9,10],[0,8,9],[5,6,10],[6,7,10],[2,7,9],[0,5,8],[1,5,7],[1,3,6],[2,4,7],[1,7,10],[0,2,10],[1,4,9],[4,6,8],[6,8,10],[0,1,9],[3,7,9],[4,7,10],[0,1,10],[6,9,11],[1,6,8],[6,9,11],[2,4,7],[2,5,8],[2,3,11],[0,2,9],[2,6,9],[2,3,8],[1,6,8],[3,4,6],[1,8,11],[3,6,9],[4,5,8],[3,10,11],[0,3,5],[1,6,8],[3,5,11],[2,3,9],[0,3,9],[2,3,5],[1,2,3],[5,8,9],[3,6,9],[3,7,9],[3,8,9],[0,4,10],[0,1,3],[8,9,11],[0,3,6],[1,4,5],[0,4,8],[5,6,8],[1,9,11],[0,4,9],[3,8,9],[2,6,10],[0,9,11],[3,10,11],[1,2,8],[5,7,8],[1,6,7],[1,9,11],[8,9,10],[2,9,11],[1,3,5],[2,8,9],[3,8,9],[7,8,11],[0,7,9],[0,1,7],[0,5,11],[5,6,9],[5,7,10],[4,5,11],[0,2,9],[5,6,10],[2,5,7],[3,4,11],[6,8,10],[0,4,9],[0,4,7],[0,2,6],[6,7,9],[7,8,9]],[[1,4,7],[1,4,10],[5,7,10],[0,3,5],[4,6,9],[1,6,9],[0,3,6],[2,5,10],[3,8,9],[3,5,7],[2,3,11],[1,2,9],[0,5,9],[1,10,11],[2,3,8],[7,9,11],[5,7,8],[2,4,10],[2,3,11],[7,9,11],[4,7,9],[0,5,11],[1,5,10],[0,1,11],[2,6,7],[3,7,9],[4,5,6],[4,6,9],[4,9,10],[3,6,9],[1,6,9],[6,7,11],[0,2,6],[3,9,11],[3,9,11],[1,6,9],[4,8,11],[0,1,5],[0,3,10],[1,9,10],[0,5,8],[3,8,9],[1,6,11],[2,4,11],[5,8,10],[1,2,10],[3,7,10],[5,9,10],[3,5,9],[0,1,8],[3,4,6],[5,6,7],[0,7,8],[1,4,6],[0,2,5],[2,5,11],[2,7,11],[3,6,11],[0,3,8],[8,10,11],[4,9,10],[0,4,9],[0,1,3],[4,5,9],[1,6,10],[5,8,9],[2,6,10],[4,8,10],[1,6,7],[3,4,10],[0,5,8],[0,8,10],[3,5,9],[4,9,10],[0,1,3],[3,10,11],[1,7,11],[2,8,11],[8,10,11],[0,6,7],[0,3,6],[0,3,5],[3,4,8],[0,4,11],[0,2,6],[2,3,7],[3,7,11],[1,2,10],[5,8,10],[0,4,9],[1,3,10],[1,3,8],[4,5,9],[0,5,7],[0,5,9],[0,5,6],[4,6,10],[1,5,11],[3,7,8],[0,2,11],[2,6,7],[6,7,11],[0,1,10],[2,3,4],[1,3,7],[3,4,5],[0,5,7],[1,5,6],[2,4,5],[0,3,5],[3,6,10],[2,5,9],[1,6,11],[1,4,8],[1,2,11],[3,10,11],[0,2,4],[0,2,7],[1,9,11],[4,8,10],[2,5,6],[2,9,11],[4,7,11],[4,9,11],[2,7,10],[2,8,11],[4,5,9],[4,5,6],[0,4,11],[0,2,5],[3,6,7],[4,6,7],[4,5,11],[3,5,10],[3,4,5],[2,7,9],[0,1,2],[3,7,10],[3,8,11],[2,4,6],[0,7,9],[6,10,11],[1,7,10],[1,4,5],[1,4,9],[0,2,7],[6,10,11],[1,5,10],[2,4,11],[6,9,11],[1,2,10],[1,2,5],[3,7,9],[0,10,11],[1,2,9],[0,4,11],[4,5,11],[1,3,9],[3,7,8],[2,6,10],[5,7,9],[1,3,7],[0,1,11],[0,7,8],[0,1,11],[3,4,8],[0,7,9],[3,5,6],[1,2,10],[5,8,11],[8,10,11],[3,6,8],[0,2,8],[4,6,8],[3,10,11],[5,9,11],[4,7,9],[9,10,11],[0,1,7],[1,3,5],[6,9,11],[3,6,10],[1,2,11],[0,5,10],[4,6,8],[3,6,10],[0,2,8],[0,7,9],[5,9,10],[3,6,11],[3,6,11],[0,2,9],[0,6,8],[4,8,11],[0,4,6],[1,5,11],[1,9,10],[6,7,8],[0,4,6],[4,6,11],[3,4,9],[2,10,11],[3,8,9],[4,5,9],[1,5,9],[0,1,6],[1,2,6],[5,7,9],[2,9,10],[2,4,11],[4,5,8],[0,4,10],[2,5,9],[2,4,6],[0,4,6],[4,8,11],[2,9,11],[0,4,7],[2,3,10],[3,9,10],[0,2,5],[0,1,2],[0,6,9],[4,7,9],[3,4,6],[2,10,11],[3,5,8],[5,8,11],[5,6,7],[4,8,9],[3,4,7],[1,2,5],[4,5,11],[2,8,11],[0,6,7],[6,10,11],[0,2,4],[5,6,8],[2,7,11],[0,4,5],[0,2,9],[4,5,10],[0,4,6],[3,4,6],[1,3,9],[2,3,5],[2,3,8],[1,4,8],[1,3,7],[2,7,11],[2,3,7],[0,5,9],[5,9,10],[1,4,8],[0,2,4],[2,8,11],[2,3,8],[1,8,10],[2,3,6],[3,6,11],[3,6,11],[0,4,10],[4,5,10],[7,9,10],[2,5,9],[3,6,7],[5,6,10],[3,8,10],[4,6,7],[6,9,10],[0,2,7],[0,2,5],[1,10,11],[2,6,11],[5,6,11],[4,5,6],[0,3,6],[0,1,3],[3,4,7],[1,8,11],[9,10,11],[0,1,6],[0,1,5],[1,4,7],[0,8,11],[0,1,7],[0,5,7],[5,6,11],[2,9,11],[0,2,6],[3,5,6],[8,9,11],[3,6,7],[4,6,9],[2,7,8],[3,7,10],[1,4,8],[0,4,6],[3,7,8],[2,7,10],[1,7,9],[3,5,10],[3,6,11],[1,5,10],[2,3,8],[3,7,8],[6,7,11],[0,8,9],[4,6,9],[2,4,10],[6,7,8],[2,3,9],[0,4,10],[0,7,10],[2,7,9],[0,4,10],[1,5,8],[3,6,9],[2,5,11],[1,6,9],[5,9,10],[1,2,9],[2,3,11],[0,1,11],[6,8,9],[4,5,6],[4,9,10],[4,6,10],[4,5,6],[6,7,10],[0,1,10],[0,6,11],[6,9,10],[4,6,7],[1,8,10],[0,6,11],[2,6,7],[0,1,11],[4,7,10],[4,8,10],[5,7,8],[1,2,11],[0,4,11],[7,8,10],[0,8,10],[2,4,5],[6,7,8],[7,8,9],[1,2,11],[0,3,5],[3,5,10],[1,7,11],[4,5,11],[4,7,9],[0,4,5],[3,4,10],[5,6,11],[0,7,11],[0,9,11],[0,7,8],[1,2,10],[0,2,6],[5,8,11],[1,10,11],[5,6,9],[1,2,11],[0,6,10],[2,3,6],[3,7,11],[1,9,10],[6,10,11],[2,6,10],[4,8,11],[6,8,11],[3,6,9],[0,8,10],[3,4,5],[1,2,3],[9,10,11],[1,2,3],[4,6,7],[1,4,10],[1,4,6],[3,4,6],[0,3,8],[3,4,10],[3,10,11],[4,6,10],[4,6,9],[2,6,7],[2,9,10],[1,9,11],[2,4,8],[5,7,10],[4,5,6],[0,5,10],[2,6,8],[5,6,8],[0,3,6],[3,5,6],[0,6,8],[3,9,10],[3,8,10],[2,6,9],[0,1,7],[5,7,9],[0,6,8],[6,9,10],[2,7,8],[3,6,11],[6,8,10],[2,8,10],[5,8,10],[2,8,11],[1,3,6],[5,8,9],[6,8,9],[2,3,8],[0,7,10],[1,4,5],[5,6,7],[5,6,9],[3,8,11],[2,4,9],[3,4,6],[3,5,6],[3,6,8],[2,4,6],[3,4,8],[3,7,8],[4,8,9],[5,7,8],[0,6,7],[1,6,10],[6,8,11],[3,5,11],[1,3,7],[0,5,9],[1,3,4],[7,9,10],[2,6,11],[4,5,11],[7,9,11],[0,5,8],[5,6,11],[0,3,9],[0,6,10],[0,3,11],[0,7,8],[3,6,10],[3,7,11],[2,5,7],[0,3,7],[1,5,11],[0,10,11],[4,10,11],[5,8,10],[7,8,9],[3,4,9],[5,8,9],[3,6,8],[2,5,8],[2,4,8],[4,6,10],[6,9,11],[4,5,11],[0,3,5],[4,6,7],[2,9,11],[1,4,10],[1,5,6],[1,2,10],[0,1,6],[0,5,6],[0,5,7],[1,3,6],[1,5,10],[1,5,9],[3,5,6],[1,10,11],[3,8,11],[0,8,10],[3,5,6],[2,3,5],[0,2,3],[0,3,5],[0,2,8],[7,8,9],[1,7,9],[2,5,11],[1,2,5],[1,3,5],[7,9,11],[7,9,10],[5,6,7],[0,5,6],[1,5,9],[1,3,5],[5,6,10],[3,9,10],[0,4,5],[1,3,8],[0,5,10],[2,5,9],[0,1,7],[5,8,11],[7,8,11],[2,3,7],[2,3,6],[3,5,10],[0,3,10],[0,2,4]],[[0,8,9],[5,6,9],[2,3,4],[0,2,11],[3,5,6],[1,4,8],[1,4,9],[2,3,11],[2,3,8],[3,7,11],[3,5,9],[1,2,7],[1,2,8],[0,4,6],[4,5,11],[2,6,7],[2,6,8],[4,6,7],[2,3,9],[5,9,10],[3,8,9],[1,6,7],[0,2,10],[0,1,9],[7,8,9],[0,1,7],[0,2,10],[0,3,5],[3,8,9],[2,7,10],[0,5,10],[1,9,10],[2,9,10],[3,5,9],[2,5,11],[2,8,9],[7,10,11],[1,4,6],[3,10,11],[5,7,8],[2,3,8],[1,2,8],[1,7,11],[2,4,11],[0,1,5],[2,7,8],[5,7,9],[2,3,10],[4,9,11],[1,7,9],[2,3,5],[2,7,8],[2,3,9],[0,2,10],[1,3,8],[6,8,10],[0,2,4],[0,8,11],[3,7,10],[2,3,11],[6,7,10],[3,9,11],[1,3,4],[0,7,10],[4,5,8],[7,8,11],[7,8,9],[0,5,6],[0,10,11],[5,7,11],[3,6,8],[5,6,11],[2,7,11],[1,2,10],[0,4,8],[2,5,9],[2,5,11],[2,5,8],[2,5,9],[2,3,11],[0,5,11],[1,2,4],[3,5,7],[3,5,8],[1,2,7],[3,8,10],[0,8,11],[1,2,6],[0,4,8],[0,4,9],[4,8,9],[0,6,7],[7,10,11],[1,3,4],[3,5,7],[3,4,8],[1,7,9],[2,4,10],[3,6,7],[1,6,9],[0,7,8],[3,4,8],[0,3,8],[2,4,9],[3,10,11],[0,3,6],[4,10,11],[0,2,10],[5,10,11],[0,1,5],[2,8,11],[2,3,6],[3,6,11],[3,4,5],[2,7,11],[3,6,10],[0,4,8],[0,4,10],[2,10,11],[1,3,9],[1,10,11],[3,7,10],[2,8,11],[0,4,5],[2,9,10],[3,9,10],[3,5,11],[2,5,6],[0,5,7],[1,4,10],[8,9,11],[0,4,8],[3,7,8],[7,8,10],[0,8,10],[6,7,11],[1,2,10],[1,3,5],[1,5,8],[2,3,8],[1,2,6],[0,2,9],[0,3,7],[0,4,5],[4,6,10],[8,10,11],[5,9,10],[2,6,10],[1,3,10],[1,5,6],[3,5,9],[5,8,9],[3,6,7],[0,2,8],[7,8,10],[0,3,10],[0,3,8],[5,8,10],[8,9,10],[4,7,9],[2,5,6],[2,7,8],[1,6,8],[2,3,11],[4,6,10],[8,10,11],[5,10,11],[3,6,11],[2,3,8],[1,4,10],[1,4,10],[4,5,7],[3,6,11],[0,2,8],[2,6,11],[1,6,10],[1,3,6],[6,8,10],[5,6,9],[2,7,10],[3,10,11],[4,8,11],[7,8,9],[0,2,11],[6,8,11],[1,2,8],[1,2,4],[1,2,4],[0,5,11],[0,2,9],[0,1,8],[2,4,11],[1,10,11],[1,2,7],[1,9,10],[4,6,11],[2,6,8],[1,3,10],[4,9,11],[0,5,11],[0,1,8],[1,3,8],[1,5,6],[0,3,9],[0,4,11],[3,4,7],[0,1,10],[0,4,8],[1,3,11],[4,6,10],[1,3,9],[0,4,11],[8,9,10],[3,9,11],[0,2,9],[4,7,11],[0,4,7],[2,9,11],[0,9,10],[2,8,11],[2,4,6],[3,7,10],[2,5,9],[5,9,11],[0,7,8],[8,10,11],[5,8,10],[3,8,10],[2,8,9],[2,6,11],[5,9,11],[4,8,10],[6,10,11],[5,7,11],[7,8,11],[0,5,10],[1,2,11],[1,4,9],[0,3,4],[3,4,6],[1,9,11],[0,2,3],[7,8,11],[2,4,9],[9,10,11],[0,9,10],[0,7,8],[3,7,9],[7,10,11],[3,6,7],[0,7,10],[4,5,11],[0,7,11],[4,9,10],[6,9,11],[0,1,5],[1,4,9],[1,2,9],[3,5,11],[5,8,10],[0,4,11],[0,2,6],[0,2,9],[3,4,10],[7,8,9],[2,8,9],[0,5,7],[0,1,2],[3,8,11],[4,7,10],[0,1,10],[4,6,11],[0,3,9],[3,5,8],[9,10,11],[5,10,11],[0,6,10],[0,3,8],[2,4,7],[0,2,11],[3,5,10],[2,10,11],[1,5,10],[5,9,11],[0,1,5],[1,2,6],[5,9,10],[0,1,11],[0,1,5],[1,9,10],[1,5,11],[2,5,9],[5,7,10],[2,8,11],[1,2,10],[3,5,8],[3,5,11],[3,4,11],[0,2,9],[1,9,10],[0,3,4],[2,5,8],[3,4,8],[0,4,5],[1,6,10],[2,3,9],[0,1,11],[1,9,10],[0,1,3],[3,8,10],[2,7,11],[1,2,3],[1,2,8],[0,5,11],[2,6,10],[1,2,8],[5,6,7],[1,8,11],[1,7,9],[0,2,11],[1,5,11],[2,8,10],[5,9,11],[4,10,11],[2,3,10],[2,6,9],[0,10,11],[3,4,11],[1,7,11],[0,3,7],[0,2,11],[1,3,6],[2,5,8],[0,5,6],[1,10,11],[1,4,6],[1,4,6],[1,2,4],[2,6,10],[2,3,10],[6,7,11],[1,2,10],[1,2,7],[2,3,7],[0,2,4],[1,4,9],[2,8,10],[0,3,6],[2,7,11],[1,8,11],[2,4,9],[5,8,10],[4,5,9],[4,10,11],[2,10,11],[4,10,11],[3,7,10],[8,10,11],[0,6,9],[0,5,11],[1,6,10],[1,5,7],[2,4,8],[3,5,8],[5,10,11],[5,7,9],[0,1,9],[5,9,11],[0,8,10],[0,3,7],[7,9,11],[2,4,9],[2,4,5],[3,8,10],[4,6,7],[0,5,6],[4,8,10],[5,8,11],[0,6,9],[1,2,10],[1,2,8],[5,7,10],[1,2,7],[6,7,9],[1,4,7],[5,9,10],[1,2,4],[4,10,11],[4,5,11],[2,8,11],[3,6,10],[0,5,10],[1,3,8],[1,4,7],[0,6,7],[1,5,7],[3,6,8],[1,7,11],[0,1,3],[2,4,5],[3,7,10],[0,7,9],[0,5,11],[0,3,10],[4,5,11],[4,6,9],[1,4,9],[4,5,6],[4,5,11],[5,7,11],[3,5,10],[0,9,11],[1,7,10],[7,8,9],[5,8,9],[2,4,7],[3,10,11],[2,6,7],[5,7,9],[4,5,8],[6,9,10],[0,5,6],[2,6,10],[0,7,8],[5,7,11],[6,7,9],[3,5,6],[0,3,4],[2,7,8],[4,7,9],[1,10,11],[1,9,11],[1,10,11],[1,5,8],[2,3,11],[0,6,8],[4,8,10],[4,7,8],[0,6,7],[2,5,8],[4,5,10],[1,2,4],[4,8,10],[2,4,9],[1,3,10],[4,9,10],[3,5,9],[3,7,11],[2,8,11],[7,9,11],[5,6,9],[3,7,8],[4,6,8],[0,1,8],[0,3,11],[1,3,8],[6,7,11],[0,1,4],[2,9,10],[8,10,11],[1,4,8],[1,4,11],[2,5,6],[1,6,10],[5,8,11],[3,7,9],[0,7,9],[0,1,4],[1,3,9],[0,7,9],[2,5,10],[1,4,10],[0,4,10],[3,8,9],[0,5,9],[2,4,8],[3,4,10],[2,6,10],[1,2,5],[3,6,7],[1,4,7],[6,7,9],[5,9,10],[0,1,8],[5,8,10],[1,5,7],[0,7,11],[1,9,11],[4,6,9],[0,2,9],[2,3,4],[4,7,8],[4,7,10],[4,8,11],[2,4,6],[0,8,10],[0,3,4],[0,4,6],[4,8,11],[6,7,9],[0,1,9],[1,3,10],[3,4,10],[1,6,11],[0,4,9],[0,1,6],[5,8,11],[0,2,7],[3,6,10],[0,6,8],[4,9,10],[2,10,11]],[[1,2,8],[1,4,6],[1,4,11],[4,8,9],[1,4,7],[2,3,9],[1,9,10],[3,4,11],[1,3,10],[5,8,11],[4,5,8],[5,6,8],[5,6,8],[7,9,10],[2,5,8],[5,9,11],[1,6,10],[3,8,10],[5,7,8],[2,5,10],[0,7,11],[6,7,10],[0,7,10],[5,10,11],[0,3,7],[2,6,7],[4,7,11],[1,7,11],[3,8,11],[1,2,8],[3,5,9],[1,6,11],[0,9,10],[3,9,10],[3,7,8],[2,3,10],[5,9,10],[2,4,10],[0,4,5],[0,4,9],[1,6,11],[0,5,6],[2,8,10],[0,3,10],[1,7,11],[2,3,9],[0,5,8],[0,7,9],[1,4,5],[2,3,7],[0,3,7],[5,6,9],[4,6,9],[3,4,7],[1,6,10],[3,9,10],[1,2,9],[4,8,10],[0,1,7],[2,4,6],[6,10,11],[1,4,9],[7,10,11],[3,4,6],[7,8,9],[3,6,10],[3,4,8],[3,4,5],[0,8,10],[6,8,11],[1,3,10],[0,2,9],[2,7,11],[0,3,11],[2,4,7],[0,3,11],[2,6,11],[3,5,6],[2,7,10],[6,8,11],[1,2,5],[4,5,8],[6,7,11],[4,10,11],[2,4,6],[0,1,8],[2,4,6],[8,10,11],[0,4,8],[2,4,5],[1,6,7],[4,9,11],[2,9,10],[3,8,10],[1,8,9],[3,4,9],[0,1,10],[1,9,10],[3,6,8],[1,2,5],[3,7,8],[2,3,9],[0,4,10],[0,6,11],[0,1,7],[2,8,11],[0,6,9],[1,9,11],[3,6,7],[1,6,7],[1,5,8],[0,7,9],[7,9,10],[5,8,11],[0,9,11],[2,6,9],[2,3,5],[6,10,11],[6,7,9],[3,4,7],[1,6,10],[4,9,10],[0,1,3],[1,4,7],[2,10,11],[0,6,7],[2,3,5],[2,3,9],[4,5,6],[3,4,9],[1,4,8],[6,8,10],[4,7,8],[0,1,4],[1,3,9],[0,6,8],[0,1,2],[0,1,5],[2,3,6],[0,2,6],[1,8,11],[1,2,3],[0,4,8],[1,5,10],[2,7,10],[1,3,8],[0,4,7],[1,6,7],[1,4,7],[2,6,11],[5,6,8],[0,4,11],[2,4,8],[0,3,7],[0,9,10],[2,3,9],[1,4,8],[1,5,10],[3,9,10],[0,5,6],[2,5,9],[2,8,10],[0,2,3],[5,6,10],[5,7,10],[0,10,11],[6,7,8],[4,6,7],[1,3,11],[0,8,9],[4,5,6],[3,9,11],[2,3,10],[5,6,7],[2,4,10],[1,3,5],[1,5,8],[4,5,11],[0,1,11],[1,3,8],[1,6,9],[5,6,10],[5,9,11],[2,4,5],[2,3,4],[4,5,11],[4,8,11],[0,10,11],[0,1,6],[0,7,9],[2,9,11],[1,5,8],[4,8,10],[1,7,11],[4,8,9],[5,6,10],[7,9,11],[1,6,11],[6,7,8],[1,3,5],[1,4,10],[1,9,11],[5,9,11],[1,4,7],[0,7,9],[6,8,10],[2,3,10],[5,8,9],[0,8,10],[3,10,11],[1,5,7],[2,7,10],[2,6,11],[1,10,11],[2,4,5],[2,6,8],[3,4,5],[1,3,7],[0,2,7],[5,8,9],[1,7,8],[1,4,7],[0,5,11],[0,1,9],[0,6,8],[0,2,3],[0,9,10],[0,5,8],[4,6,10],[0,1,9],[0,3,8],[0,2,7],[4,6,9],[1,5,7],[3,8,9],[3,7,8],[4,7,9],[0,1,2],[2,3,9],[0,2,3],[4,5,11],[4,7,10],[2,5,8],[2,7,9],[5,6,9],[0,3,9],[0,1,5],[0,6,7],[1,2,7],[5,6,11],[5,7,9],[4,5,8],[2,7,8],[3,6,11],[2,6,7],[4,5,9],[2,4,11],[2,8,9],[0,9,11],[1,2,8],[6,7,11],[6,10,11],[2,5,10],[1,6,9],[0,6,9],[5,7,8],[6,8,9],[3,5,8],[3,4,6],[0,1,7],[0,2,4],[6,10,11],[6,9,11],[0,8,9],[5,6,11],[4,7,10],[0,1,4],[3,6,9],[5,9,10],[4,10,11],[3,7,9],[0,3,6],[1,3,7],[3,5,11],[0,3,9],[1,2,9],[1,4,7],[0,6,8],[1,7,9],[1,2,9],[0,5,6],[4,5,9],[0,4,6],[0,2,8],[1,4,5],[1,8,11],[2,4,10],[4,6,11],[0,2,10],[1,5,10],[2,6,10],[0,2,3],[3,4,10],[6,7,8],[1,5,10],[3,6,7],[1,6,10],[1,6,10],[0,5,11],[1,8,11],[5,6,8],[1,4,11],[1,2,5],[2,7,8],[2,7,10],[1,5,6],[2,4,8],[5,7,11],[4,5,7],[3,6,9],[1,5,8],[4,6,7],[5,6,8],[0,2,7],[1,6,8],[4,5,7],[0,1,3],[2,3,9],[0,4,5],[3,5,8],[5,6,10],[1,7,9],[1,4,8],[2,7,9],[0,5,9],[7,9,10],[1,2,5],[1,6,10],[4,6,7],[4,8,11],[1,2,6],[0,3,8],[2,8,10],[1,5,7],[3,5,10],[0,6,8],[6,7,11],[2,6,11],[2,5,8],[3,7,8],[5,9,10],[6,8,11],[3,9,11],[0,4,6],[3,4,10],[0,5,9],[1,10,11],[7,9,10],[1,7,11],[8,9,10],[0,4,11],[2,7,10],[1,6,7],[6,8,9],[5,6,7],[2,8,10],[2,3,6],[0,8,10],[3,4,10],[6,7,10],[4,7,8],[3,4,7],[4,9,11],[4,6,8],[7,8,10],[3,5,10],[1,2,10],[1,5,8],[6,9,11],[1,3,5],[2,6,11],[2,4,9],[0,1,11],[3,9,11],[4,7,11],[3,4,6],[1,2,3],[2,5,9],[3,4,10],[5,7,9],[3,6,8],[0,6,8],[0,5,8],[1,4,9],[2,5,11],[5,9,10],[3,6,9],[1,5,7],[0,1,8],[4,6,9],[4,8,11],[2,4,7],[6,7,10],[1,5,8],[5,7,9],[2,9,11],[1,2,11],[3,7,9],[2,4,6],[0,1,5],[0,5,6],[4,7,9],[0,1,10],[6,8,11],[0,9,10],[1,3,10],[2,3,10],[6,7,9],[0,5,10],[4,7,11],[0,7,9],[1,4,9],[0,8,11],[4,6,11],[1,7,11],[0,1,10],[5,8,11],[0,4,9],[0,8,10],[3,7,11],[2,9,11],[3,5,9],[0,1,5],[4,9,10],[1,6,11],[0,5,9],[0,1,11],[0,9,11],[2,7,10],[3,5,9],[3,9,11],[1,4,7],[5,7,9],[1,4,7],[0,3,4],[2,8,9],[0,8,9],[2,6,11],[0,4,11],[1,5,7],[1,5,7],[2,7,9],[1,2,11],[0,4,6],[2,3,4],[0,8,10],[5,7,9],[0,1,9],[5,6,11],[4,6,8],[2,7,10],[4,6,9],[3,4,11],[4,9,10],[2,8,9],[1,6,7],[1,7,10],[3,5,7],[4,7,10],[0,5,7],[2,9,10],[2,3,6],[1,4,8],[1,6,9],[3,5,11],[5,9,10],[6,7,10],[0,9,11],[6,9,11],[1,4,5],[1,3,8],[2,5,11],[0,1,2],[6,7,11],[0,1,5],[4,10,11],[1,7,8],[5,6,10],[0,2,8],[4,6,9],[0,1,8],[9,10,11],[0,2,7],[3,7,9],[2,3,7],[0,5,11],[1,2,9],[2,7,8],[1,6,10],[1,3,7],[0,6,11],[2,3,5],[6,10,11],[1,5,7],[0,9,10],[0,4,11],[2,3,10],[2,7,10],[0,2,6],[2,7,11],[0,2,6],[0,9,11]],[[1,7,8],[0,10,11],[3,9,10],[1,7,9],[6,10,11],[2,5,7],[3,9,11],[3,7,8],[1,3,6],[5,8,10],[2,4,11],[2,10,11],[4,5,7],[3,4,6],[0,3,5],[0,2,6],[0,5,9],[0,2,11],[2,4,7],[3,5,7],[1,5,9],[0,9,10],[3,4,5],[6,8,11],[6,9,10],[2,3,4],[4,6,11],[1,2,3],[1,4,10],[3,6,10],[0,3,7],[3,7,11],[4,5,9],[2,3,4],[7,8,10],[1,4,8],[3,6,9],[0,5,9],[1,8,10],[0,8,9],[0,2,8],[0,1,4],[5,8,10],[0,8,10],[2,8,9],[7,8,10],[0,3,6],[6,7,9],[3,8,10],[2,4,7],[3,9,10],[1,5,7],[0,5,6],[4,6,9],[2,5,10],[0,6,8],[0,5,6],[0,1,4],[4,6,10],[0,7,11],[4,5,7],[1,2,7],[3,5,10],[3,4,7],[0,3,4],[1,3,4],[3,7,9],[1,7,10],[0,3,9],[4,7,11],[1,4,11],[4,8,10],[2,5,9],[5,6,11],[4,10,11],[6,7,8],[4,8,11],[4,9,11],[3,7,10],[0,1,10],[1,6,10],[4,8,10],[2,4,5],[8,10,11],[2,7,9],[7,8,9],[0,4,9],[3,5,10],[0,3,8],[5,7,11],[0,4,9],[4,8,11],[1,3,4],[3,6,10],[0,6,11],[2,7,9],[2,3,9],[3,8,10],[1,7,8],[3,6,10],[1,3,11],[2,5,6],[0,1,7],[3,5,7],[2,7,8],[3,6,9],[4,5,8],[4,8,9],[0,5,11],[4,9,10],[0,2,6],[0,4,7],[4,5,10],[0,3,11],[0,2,10],[4,6,8],[5,6,8],[0,7,9],[1,2,7],[1,3,4],[2,4,8],[3,7,11],[1,4,10],[3,8,9],[5,7,8],[0,1,6],[4,8,11],[0,2,7],[3,4,6],[3,4,6],[4,8,10],[3,7,11],[0,2,6],[3,6,10],[2,5,8],[5,6,9],[3,9,10],[0,1,2],[5,8,11],[0,3,11],[4,8,10],[2,6,7],[0,6,10],[0,5,11],[3,6,8],[9,10,11],[1,5,7],[7,8,11],[4,7,9],[0,4,10],[3,7,11],[0,5,7],[1,9,10],[4,6,11],[0,4,6],[0,3,8],[0,1,5],[1,3,10],[1,10,11],[0,5,10],[1,2,6],[1,2,8],[3,7,11],[8,9,10],[3,6,10],[2,6,10],[1,4,7],[0,6,8],[0,1,4],[0,6,7],[2,7,9],[1,2,9],[5,7,9],[1,6,10],[0,2,6],[2,4,5],[0,3,4],[4,8,10],[3,6,7],[2,5,6],[1,6,11],[5,6,10],[0,5,11],[1,7,9],[2,6,8],[0,4,9],[3,4,5],[1,6,8],[0,1,10],[2,5,10],[0,3,7],[0,4,6],[1,2,3],[3,9,10],[1,2,5],[3,8,10],[2,8,11],[4,5,6],[2,5,6],[0,2,11],[5,6,9],[0,1,6],[1,2,11],[1,8,9],[2,4,11],[1,2,9],[1,5,11],[0,4,11],[1,4,7],[2,8,9],[0,6,7],[3,6,7],[0,3,7],[2,6,9],[0,2,8],[2,7,8],[0,4,8],[1,2,6],[2,4,10],[0,9,11],[2,3,5],[2,7,10],[4,5,9],[0,3,9],[4,5,6],[4,6,7],[1,3,9],[1,3,9],[1,5,7],[0,1,2],[2,10,11],[0,3,11],[0,3,6],[1,2,8],[0,6,9],[3,5,10],[5,7,9],[2,5,10],[1,4,9],[1,6,10],[4,9,11],[0,5,10],[3,4,7],[3,8,11],[1,9,10],[3,7,9],[4,6,8],[0,1,2],[4,5,8],[1,3,7],[4,5,11],[1,3,5],[6,9,11],[2,4,10],[6,8,11],[2,4,9],[4,6,9],[4,7,9],[3,10,11],[2,4,6],[4,5,6],[1,2,10],[0,2,11],[4,10,11],[1,5,8],[6,9,11],[2,6,10],[2,6,10],[1,7,8],[5,7,9],[0,9,11],[0,4,7],[1,10,11],[0,7,10],[3,6,7],[6,8,11],[6,8,9],[7,8,11],[1,5,9],[0,1,8],[0,4,9],[6,8,10],[1,3,9],[0,6,9],[5,6,7],[4,5,9],[3,8,9],[7,8,10],[3,5,9],[0,1,5],[2,3,10],[4,5,7],[2,7,11],[2,4,6],[1,2,7],[2,9,11],[0,7,11],[9,10,11],[1,7,10],[0,5,11],[1,5,8],[1,5,6],[0,5,7],[3,7,8],[2,3,7],[1,2,4],[1,4,7],[3,10,11],[2,8,9],[1,5,11],[0,3,10],[1,2,3],[5,10,11],[0,1,11],[0,2,4],[2,3,5],[0,3,8],[1,9,10],[7,9,11],[6,7,8],[3,4,8],[7,8,9],[7,9,11],[2,8,11],[3,4,7],[7,9,11],[2,5,7],[2,4,7],[0,7,9],[0,2,9],[4,7,10],[8,10,11],[0,4,10],[0,6,9],[0,1,11],[3,6,11],[0,5,6],[7,8,9],[1,3,7],[1,4,7],[0,1,10],[2,5,9],[0,4,11],[0,7,9],[0,5,9],[3,6,8],[1,5,6],[2,5,9],[4,9,11],[3,5,10],[0,6,10],[0,7,9],[3,8,9],[1,7,11],[5,8,11],[1,3,8],[5,7,9],[3,5,11],[2,7,8],[7,9,10],[2,3,7],[2,3,7],[5,6,10],[0,3,6],[1,2,10],[4,8,9],[2,3,8],[0,2,9],[0,2,3],[4,7,10],[2,6,7],[1,4,9],[4,10,11],[0,4,9],[2,4,10],[5,9,10],[4,6,11],[3,6,8],[8,9,10],[2,5,11],[1,2,8],[1,6,11],[4,7,11],[1,2,4],[5,6,11],[0,1,8],[8,10,11],[2,4,8],[5,8,10],[1,9,11],[8,10,11],[1,5,9],[0,9,10],[7,9,11],[6,7,9],[0,3,6],[5,7,8],[3,8,11],[0,2,8],[4,7,8],[5,6,11],[1,2,11],[3,6,7],[1,6,10],[3,4,5],[8,9,11],[2,8,11],[6,7,8],[1,5,11],[1,3,5],[1,2,4],[4,6,8],[0,1,11],[0,7,10],[4,7,11],[5,8,11],[2,8,9],[8,9,11],[3,5,10],[8,9,10],[5,8,9],[3,5,10],[8,10,11],[6,7,11],[0,1,5],[2,5,11],[0,5,9],[0,5,8],[0,5,11],[0,2,11],[7,8,10],[0,1,8],[1,5,11],[3,6,11],[2,6,7],[0,1,3],[1,8,9],[1,5,7],[2,8,9],[5,7,8],[1,2,3],[1,5,9],[2,6,9],[4,10,11],[1,10,11],[5,7,8],[6,7,10],[2,4,11],[0,3,10],[1,3,11],[0,3,5],[0,1,4],[0,5,6],[1,5,11],[0,3,5],[0,2,3],[4,8,9],[5,9,10],[1,2,11],[1,7,11],[7,10,11],[2,9,10],[3,7,8],[3,5,9],[3,4,9],[0,8,11],[3,5,8],[3,8,9],[0,1,7],[1,5,11],[1,9,10],[7,9,10],[0,3,4],[2,5,6],[6,7,11],[3,6,7],[1,6,7],[0,6,10],[4,8,11],[1,5,9],[1,5,10],[0,4,5],[0,2,5],[7,8,9],[1,4,8],[5,6,11],[1,2,4],[2,5,7],[5,7,9],[1,3,6],[7,9,10],[1,8,11],[4,7,10],[6,9,10],[1,2,6],[5,8,11],[0,8,10],[1,8,10],[1,3,8],[5,9,10],[0,10,11],[0,9,11],[4,6,9],[2,5,10],[8,10,11],[3,4,10],[0,4,9],[2,9,10],[1,2,7],[1,3,7],[2,3,10],[0,2,9]],[[3,4,10],[3,9,11],[3,7,8],[7,9,11],[3,6,7],[0,2,6],[3,5,10],[6,7,11],[2,5,10],[1,7,8],[1,5,11],[1,3,4],[0,7,11],[2,4,11],[0,2,10],[1,2,9],[6,9,11],[7,8,10],[2,6,10],[1,2,8],[2,5,8],[2,10,11],[2,3,7],[7,10,11],[1,3,11],[4,7,10],[4,6,10],[2,4,9],[1,3,8],[0,2,5],[1,2,6],[2,6,8],[4,6,10],[7,10,11],[0,2,7],[2,3,4],[5,7,10],[1,5,6],[0,1,9],[2,3,6],[1,6,9],[3,5,8],[0,2,8],[3,4,6],[1,5,11],[0,3,10],[3,8,9],[1,4,11],[1,3,9],[2,5,10],[7,9,11],[1,6,7],[0,1,3],[0,5,10],[0,5,8],[8,10,11],[7,8,11],[7,10,11],[2,7,8],[0,7,11],[1,3,10],[1,8,9],[2,3,6],[8,9,11],[1,3,5],[0,6,8],[3,5,10],[2,8,10],[0,1,5],[0,3,11],[0,2,10],[0,1,5],[7,8,10],[0,4,8],[3,5,8],[4,8,11],[3,5,10],[0,4,9],[1,5,11],[3,6,11],[9,10,11],[4,7,11],[7,8,9],[2,3,10],[5,6,9],[3,8,9],[2,3,9],[0,8,11],[0,3,4],[0,6,11],[1,4,6],[2,6,7],[0,10,11],[1,4,9],[2,8,11],[0,3,4],[2,6,9],[1,2,7],[6,10,11],[0,2,3],[2,10,11],[2,4,10],[1,5,10],[6,7,11],[0,6,9],[0,5,10],[1,3,6],[0,8,9],[4,5,8],[0,2,7],[1,2,9],[5,7,8],[3,9,11],[1,2,9],[2,5,11],[1,2,11],[6,7,9],[3,8,10],[3,5,8],[0,6,9],[5,9,11],[0,1,7],[2,8,11],[2,3,6],[2,6,10],[2,6,8],[1,8,11],[4,8,10],[4,8,11],[2,8,9],[1,10,11],[3,5,7],[2,7,10],[2,4,8],[6,7,11],[4,5,10],[1,6,9],[2,3,9],[2,5,11],[0,5,7],[1,7,9],[3,10,11],[2,8,10],[0,5,6],[0,3,6],[1,4,10],[2,6,11],[4,5,9],[0,3,7],[0,7,11],[1,4,10],[0,5,7],[2,3,6],[6,7,10],[0,4,8],[4,6,8],[0,3,6],[2,5,10],[1,7,11],[2,7,10],[1,6,7],[1,3,6],[0,3,10],[1,4,6],[5,9,11],[5,9,11],[0,2,3],[6,8,11],[4,6,8],[0,1,2],[4,6,11],[1,3,6],[2,4,6],[1,5,10],[2,6,9],[3,4,8],[2,3,7],[2,6,10],[4,6,7],[2,4,11],[6,10,11],[5,9,10],[5,6,10],[1,2,6],[2,6,8],[0,3,6],[5,6,10],[0,4,11],[5,6,7],[3,6,10],[1,5,11],[8,10,11],[1,7,8],[7,9,11],[2,5,6],[1,8,10],[0,4,7],[0,4,8],[3,4,5],[0,9,10],[2,7,10],[0,1,5],[0,5,8],[4,7,8],[2,4,6],[1,7,8],[0,2,3],[2,3,4],[0,3,9],[2,7,9],[0,1,2],[2,3,11],[0,2,7],[4,7,11],[3,8,11],[0,1,11],[3,7,9],[3,6,8],[1,8,9],[0,5,7],[1,2,6],[1,3,8],[6,9,11],[1,5,8],[7,9,10],[0,2,3],[2,4,6],[4,6,9],[1,3,11],[3,7,8],[1,5,9],[5,6,11],[2,3,8],[3,5,6],[1,4,9],[3,7,11],[5,8,11],[6,10,11],[4,8,10],[2,4,7],[4,10,11],[2,10,11],[0,2,8],[5,8,10],[1,8,9],[1,8,9],[1,3,7],[2,7,9],[2,4,10],[3,6,7],[0,8,11],[5,8,11],[0,2,6],[0,1,10],[0,4,6],[2,6,11],[3,4,5],[1,2,4],[1,3,11],[1,4,9],[2,4,7],[1,8,10],[2,3,7],[2,5,6],[5,8,9],[3,8,11],[2,3,8],[1,4,8],[1,5,11],[0,6,7],[1,2,7],[0,2,9],[0,8,11],[0,1,9],[2,3,10],[4,5,9],[2,3,10],[0,5,7],[0,9,11],[0,3,8],[3,5,6],[3,7,11],[6,7,10],[2,3,7],[4,7,10],[2,6,11],[0,4,11],[5,7,8],[4,5,6],[0,2,4],[0,3,7],[5,6,8],[6,7,9],[0,1,7],[8,9,11],[1,2,5],[0,2,9],[1,6,11],[4,5,10],[5,9,11],[1,3,7],[1,5,9],[3,6,10],[1,5,8],[3,5,9],[4,7,9],[0,6,9],[9,10,11],[0,5,6],[3,4,9],[2,5,8],[0,3,11],[5,9,11],[2,3,4],[3,4,5],[2,4,6],[3,8,10],[3,8,11],[6,8,11],[1,3,8],[3,7,9],[1,10,11],[0,5,7],[0,3,10],[3,5,6],[1,5,9],[0,3,10],[1,8,9],[2,6,8],[0,6,10],[2,3,6],[1,7,10],[6,7,9],[7,9,10],[1,6,10],[0,9,11],[1,6,11],[4,5,11],[2,3,9],[0,7,10],[1,2,4],[1,3,4],[0,1,11],[0,4,5],[3,7,11],[5,6,10],[6,10,11],[6,8,10],[2,5,7],[0,9,11],[2,4,11],[3,4,11],[4,7,9],[1,9,11],[0,5,6],[2,5,7],[5,7,8],[3,6,10],[1,2,10],[1,7,9],[0,4,9],[5,6,8],[2,4,6],[5,8,9],[1,4,9],[0,9,10],[5,6,11],[0,1,6],[8,9,11],[2,4,6],[2,8,10],[2,8,10],[0,2,6],[0,3,11],[0,5,9],[5,6,7],[3,5,11],[2,7,11],[0,2,4],[1,2,9],[4,6,10],[3,7,9],[0,2,5],[0,1,4],[2,5,6],[3,7,9],[4,5,10],[2,3,9],[2,6,9],[3,7,11],[0,1,2],[0,2,9],[2,7,10],[5,8,10],[5,7,10],[6,7,10],[4,7,9],[8,9,10],[3,5,11],[1,4,9],[3,4,5],[1,9,10],[1,3,11],[3,10,11],[3,8,11],[2,5,7],[3,9,11],[0,2,6],[4,7,8],[2,5,9],[0,2,9],[0,10,11],[3,7,8],[1,4,8],[3,5,10],[3,5,11],[0,8,10],[2,4,5],[0,4,10],[1,8,9],[0,8,9],[1,5,10],[3,6,11],[4,5,6],[2,4,6],[1,2,6],[2,7,10],[0,3,9],[1,2,3],[2,6,11],[2,5,8],[4,8,11],[3,4,7],[0,1,7],[3,6,9],[3,7,11],[3,7,9],[1,3,8],[0,2,4],[1,2,8],[1,3,6],[1,6,11],[2,8,10],[1,3,8],[3,5,10],[7,9,10],[0,5,11],[2,8,11],[5,6,9],[2,4,6],[1,2,5],[3,6,7],[2,7,10],[1,9,10],[4,6,10],[5,7,10],[0,6,11],[1,2,3],[1,4,6],[1,2,10],[2,5,7],[0,2,6],[7,9,11],[2,5,7],[0,7,10],[0,3,7],[4,6,11],[1,3,7],[5,9,11],[2,3,11],[3,4,10],[0,1,10],[6,8,10],[7,8,10],[1,4,11],[0,2,8],[2,7,10],[6,10,11],[2,8,10],[3,4,9],[2,7,9],[1,3,5],[1,8,11],[0,9,10],[1,7,9],[1,4,5],[3,5,7],[9,10,11],[0,3,10],[1,7,11],[3,6,8],[5,6,8],[1,2,3],[1,8,9],[1,5,11],[5,8,9],[0,2,11],[3,6,7],[5,7,11],[1,6,11],[0,1,2],[5,8,10],[1,5,9],[0,5,9],[0,2,8],[5,6,10],[3,7,10],[2,5,7],[0,4,9],[3,4,10],[1,6,7],[0,7,9]]]
def setup_inputs(rng):
    return {"x": rng.standard_normal((N, 128, TOK), dtype=np.float32).astype(ml_dtypes.bfloat16), "gate": (0.5 * rng.integers(1, 4, size=(N, K, TOK)) * (2 * rng.integers(0, 2, size=(N, K, TOK)) - 1)).astype(np.float32).astype(ml_dtypes.bfloat16), "w1": (rng.standard_normal((N, 128, FT * 128), dtype=np.float32) / 8).astype(ml_dtypes.bfloat16), "w2": (rng.standard_normal((N, 128, FT * 128), dtype=np.float32) / 8).astype(ml_dtypes.bfloat16)}
def setup_inputs_big(rng):
    d = setup_inputs(rng)
    for k in ("x", "gate", "w1", "w2"): d[k] = (d[k].astype(np.float32) * 1024.0).astype(d[k].dtype)
    return d
def setup_inputs_small(rng):
    d = setup_inputs(rng)
    for k in ("x", "gate", "w1", "w2"): d[k] = (d[k].astype(np.float32) * (1 / 1024.0)).astype(d[k].dtype)
    return d
def setup_inputs_apart(rng):
    d = setup_inputs(rng)
    f = (10.0 ** rng.permutation(np.linspace(-1.5, 1.5, N))).astype(np.float32).reshape(N, 1, 1)
    for k in ("x", "gate", "w1", "w2"): d[k] = (d[k].astype(np.float32) * f).astype(d[k].dtype)
    return d
def reference(x, gate, w1, w2):
    X, GATE, W1, W2 = x.astype(np.float64), gate.astype(np.float64), w1.astype(np.float64), w2.astype(np.float64)
    y = np.zeros((N, 128, TOK))
    for r in range(N):
        for t in range(TOK):
            for i, e in enumerate(ROUTE[r][t]):
                hid = np.maximum(W1[e].T @ X[r][:, t], 0.0)
                y[r][:, t] += GATE[r][i, t] * sum(W2[e][:, 128 * f:128 * f + 128].T @ hid[128 * f:128 * f + 128] for f in range(FT))
    return {"y": y.astype(ml_dtypes.bfloat16)}

@@ -1,0 +1,364 @@
+import numpy as np
+from concourse.bass import DstId, RemoteDMATransfer
+from concourse.mybir import AluOpType
+
+N = 12
+TOK = 512
+NH = TOK // 2
+NE = 11
+NB = 2 * NE + 1
+NG = 4
+NC = NH // NG
+NV = NC + NB
+GX = 16
+BIG = 4.0
+NSIM = 112
+ND = 3
+ARRIVE = [1, 2, 4, 3, 5]
+NA = 6
+NHB = 4
+FAR = True
+
+SCRATCH = {"wd": ("dram", [128, 256], "bfloat16"), "land": ("dram", [N, 128, 256], "bfloat16"),
+           "ef": ("sbuf", [128, 2, 828], "bfloat16")}
+for nm, w in (("xs", TOK + GX), ("part", TOK), ("wsb", N * 256), ("hid", N * TOK), ("hg", N * TOK), ("zt", TOK),
+              ("st", N * 128), ("ms", NH), ("et", 72), ("cg", 36), ("gt", TOK), ("tt", TOK), ("gm", TOK), ("ysb", TOK)):
+    SCRATCH[nm] = ("sbuf", [128, w], "bfloat16")
+for nm, w in (("vt", NV), ("m1", NH), ("m2", NH), ("a1", NH), ("a2", NH)):
+    SCRATCH[nm] = ("sbuf", [128, w], "float32")
+for nm in ("py", "pa", "pg0", "pg1", "ph0", "ph1", "ph2", "ph3"):
+    SCRATCH[nm] = ("psum", [128, TOK], "float32")
+SEMAPHORES = ["ldw", "ldx", "ldo", "ldg", "le", "st", "sent", "pv", "vs", "xa", "pp", "vc", "ve",
+              "hm", "rl", "gb", "ml", "ym", "yc", "du", "da", "dm", "dq", "dt", "dp", "dg"] + ["w%d" % e for e in range(N)]
+
+
+def bits(m):
+    return bin(m).count("1")
+
+
+def values(route):
+    out = []
+    for j in range(NH):
+        v = 1 << (2 * NE)
+        for h in range(2):
+            for e in route[h * NH + j]:
+                if e < NE:
+                    v |= 1 << (NE * h + e)
+        out.append(v + 0.5)
+    return out, [2.0 ** -(b + 1) for b in range(NB)]
+
+
+def plan(T, topo):
+    cores = list(T.cores)
+    chips = []
+    for c in cores:
+        if topo.chip(c) not in chips:
+            chips.append(topo.chip(c))
+    nc = len(chips)
+    on = [[r for r in range(N) if topo.chip(cores[r]) == ch] for ch in chips]
+    helpers = [[c for c in range(NSIM) if topo.chip(c) == ch and c not in cores] for ch in chips]
+    relay, relay_of, asst, asst_of, fans = {}, {}, {}, {}, []
+    fillers = [[] for r in range(N)]
+    for i in range(nc):
+        free = list(helpers[i])
+        rel = []
+        for r in on[i]:
+            cand = [h for h in free if topo.die(h) != topo.die(cores[r]) and all(topo.may_write(h, d) for d in cores)]
+            relay[r] = cand[0]
+            relay_of[cand[0]] = r
+            rel.append(cand[0])
+            free.remove(cand[0])
+        if NA:
+            for r in on[i]:
+                cand = [h for h in free if topo.die(h) == topo.die(cores[r])] + free
+                asst[r] = cand[0]
+                asst_of[cand[0]] = r
+                free.remove(cand[0])
+        fans.append(free + rel)
+        for q, h in enumerate(free + rel):
+            fillers[on[i][q % len(on[i])]].append(h)
+    if FAR:
+        idle = [c for c in range(NSIM) if topo.chip(c) not in chips]
+        idle.sort(key=lambda c: sum(1 for d in cores if topo.may_write(c, d)))
+        for c in idle:
+            ok = [r for r in range(N) if topo.may_write(c, cores[r])]
+            r = min(ok, key=lambda q: len(fillers[q]))
+            fillers[r].append(c)
+    paint = {}
+    wt = [NG] * NC + [1] * NB
+    for r in range(N):
+        k, a, acc, tot = len(fillers[r]), 0, 0, sum(wt)
+        for s, h in enumerate(fillers[r]):
+            b = a
+            while b < NV and (s == k - 1 or acc + wt[b] <= tot * (s + 1) / k + 1e-9):
+                acc += wt[b]
+                b += 1
+            if b > a:
+                paint[h] = (r, a, b)
+            a = b
+    order, landing, fan = [], {}, {}
+    for i in range(nc):
+        arr = [e for k in ARRIVE for e in on[(i - k) % nc]]
+        order.append(arr)
+        for p, e in enumerate(arr):
+            h = fans[i][p % len(fans[i])]
+            landing[(e, i)] = h
+            fan.setdefault(h, []).append(e)
+    return {"cores": cores, "chips": chips, "on": on, "relay": relay, "relay_of": relay_of, "paint": paint,
+            "order": order, "landing": landing, "fan": fan, "nc": nc, "asst": asst, "asst_of": asst_of}
+
+
+def masks(topo, P, r):
+    c = P["cores"][r]
+    far = [d for d in P["cores"] if topo.chip(d) != topo.chip(c)][0]
+    near = [d for d in P["cores"] if topo.chip(d) == topo.chip(c) and d != c][0]
+    off = topo.mask(c, far)
+    return off, topo.mask(c, near) & ~off
+
+
+def team(P, r):
+    return [P["cores"][r]] + ([P["asst"][r]] if NA else [])
+
+
+def did(topo, c):
+    rid, pid, se = topo.addr(c)
+    return DstId(rid=rid, pnc=pid)
+
+
+def send(g, T, topo, src, dsts, out_ap, in_ap, rsem, sent, m=None):
+    if m is None:
+        m = topo.mask(src, dsts[0])
+    g.remote_dma_fused([RemoteDMATransfer(dst_ids=[did(topo, c) for c in dsts], dma_engine_mask=m, remote_sem=rsem,
+                                          srcs=[in_ap], dsts=[out_ap for c in dsts], alu_op=0)], local_sem=T.sem.sent)
+    sent[0] += bits(m)
+
+
+def run_helper(g, core, T, topo, P):
+    sent = [0]
+    S = T.sem
+    job = P["paint"].get(core)
+    if job is not None:
+        vals, scales = values(T.tables["ROUTE"][job[0]])
+        n = 0
+        for c in range(job[1], job[2]):
+            if c < NC:
+                for q in range(NG):
+                    g.vector.memset(T.vt[32 * q:32 * q + 32, c:c + 1], vals[q * NC + c]).then_inc(S.pv, 1)
+                    n += 1
+            else:
+                g.vector.memset(T.vt[:, c:c + 1], scales[c - NC]).then_inc(S.pv, 1)
+                n += 1
+        g.wait_ge(S.pv, n)
+        send(g, T, topo, core, team(P, job[0]), T.vt[:, job[1]:job[2]], T.vt[:, job[1]:job[2]], S.vs, sent)
+    r = P["relay_of"].get(core)
+    if r is not None:
+        ci = P["chips"].index(topo.chip(core))
+        g.wait_ge(S["w%d" % r], bits(masks(topo, P, r)[1]))
+        for k in range(ND + 1, P["nc"]):
+            send(g, T, topo, core, [P["landing"][(r, (ci + k) % P["nc"])]], T.land[r], T.land[r], S["w%d" % r], sent)
+    for e in P["fan"].get(core, []):
+        ci = P["chips"].index(topo.chip(core))
+        g.wait_ge(S["w%d" % e], bits(topo.mask(P["cores"][e], core)))
+        early = P["order"][ci].index(e) < NA
+        tg = [P["asst"][q] if early else P["cores"][q] for q in P["on"][ci]]
+        send(g, T, topo, core, tg, T.wsb[:, e * 256:(e + 1) * 256], T.land[e], S["w%d" % e], sent)
+    g.wait_ge(S.sent, sent[0])
+
+
+def run_compute(g, core, r, T, topo, P):
+    S = T.sem
+    V, PE, SY, SC = g.vector, g.tensor, g.sync, g.scalar
+    ci = P["chips"].index(topo.chip(core))
+    nc = P["nc"]
+    boss = core == P["cores"][r]
+    sib = [q for q in P["on"][ci] if q != r][0]
+    order = ([r, sib] + P["order"][ci][NA:]) if boss else P["order"][ci][:NA]
+    L = len(order)
+    pre = 2 if boss else 0
+    off, upper = masks(topo, P, r)
+    A = AluOpType
+    sent = [0]
+
+    if boss:
+        SY.dma_start(T.wd[:, 0:128], T.w1[:, :]).then_inc(S.ldw, 16)
+        SC.dma_start(T.wd[:, 128:256], T.w2[:, :]).then_inc(S.ldw, 16)
+        SY.dma_start(T.xs[:, 0:TOK], T.x[:, :]).then_inc(S.ldx, 16)
+        SC.dma_start(T.xs[0:96, TOK:TOK + GX], T.gate[:, :]).then_inc(S.ldx, 16)
+        SC.dma_start(T.xs[96:128, TOK:TOK + GX], T.gate[0:1, :]).then_inc(S.ldx, 16)
+        SC.dma_start(T.wsb[:, r * 256 + 128:r * 256 + 256], T.w2[:, :]).then_inc(S.ldo, 16)
+        SY.dma_start(T.wsb[:, r * 256:r * 256 + 128], T.w1[:, :]).then_inc(S.ldo, 16)
+        SC.dma_start(T.gt[0:3, :], T.gate[:, :]).then_inc(S.ldg, 16)
+        wsem = S["w%d" % r]
+        g.wait_ge(S.ldw, 32)
+        g.remote_dma_fused([
+            RemoteDMATransfer(dst_ids=[did(topo, P["landing"][(r, (ci + 1) % nc)])], dma_engine_mask=off, remote_sem=wsem,
+                              srcs=[T.wd[:, :]], dsts=[T.land[r]], alu_op=0),
+            RemoteDMATransfer(dst_ids=[did(topo, P["relay"][r]), did(topo, P["cores"][sib])], dma_engine_mask=upper,
+                              remote_sem=wsem, srcs=[T.wd[:, :]],
+                              dsts=[T.land[r], T.wsb[:, r * 256:(r + 1) * 256]], alu_op=0)], local_sem=S.sent)
+        sent[0] += bits(off) + bits(upper)
+        for k in range(2, ND + 1):
+            send(g, T, topo, core, [P["landing"][(r, (ci + k) % nc)]], T.land[r], T.wd[:, :], wsem, sent)
+            if k == 2:
+                g.wait_ge(S.ldx, 48)
+                if NA:
+                    send(g, T, topo, core, [P["asst"][r]], T.xs[:, :], T.xs[:, :], S.xa, sent, upper)
+    else:
+        SY.wait_ge(S.xa, bits(upper))
+        SY.dma_start(T.gt[0:3, :], T.xs[0:96, TOK:TOK + GX]).then_inc(S.ldg, 16)
+
+    nv, ne = [0], [0]
+
+    def fc(ap, val):
+        V.memset(ap, val).then_inc(S.vc, 1)
+        nv[0] += 1
+
+    def fe(ap, val):
+        V.memset(ap, val).then_inc(S.ve, 1)
+        ne[0] += 1
+
+    fc(T.zt[:, :], 0.0)
+    fe(T.ef[0:1, :, :], 0.0)
+    V.wait_ge(S.ve, ne[0])
+    for k in range(3):
+        fe(T.ef[0:1, :, k:k + 751:75], BIG if k < 2 else 1.0)
+    for e1 in range(NE - 1):
+        for k in range(2):
+            a = 72 * e1 + 3 * (e1 + 1) + k
+            fe(T.ef[0:1, :, a:a + 3 * (NE - 2 - e1) + 1:3], -1.0 if k == 0 else 1.0)
+    for k in (1, 2):
+        fe(T.ef[0:1, :, 33 + k:33 + k + 721:72], -1.0)
+    fe(T.ef[0:1, 1, 756:756 + 70:3], 1.0 - BIG)
+    fe(T.ef[0:1, 1, 757:757 + 70:3], -1.0 - BIG)
+    V.wait_ge(S.ve, ne[0])
+    fe(T.ef[0:1, 1, 756 + 33:756 + 70:36], 0.0)
+    fe(T.ef[0:1, 1, 756 + 34:756 + 36], 3.0)
+    fe(T.ef[0:1, 1, 756 + 70:756 + 72], 3.0)
+    SY.wait_ge(S.ve, ne[0])
+    SY.dma_start(T.et[0:NB, :], T.ef[0:1, :, :]).then_inc(S.le, 16)
+    for ap, val in ((T.cg[0:3, :], 0.0), (T.cg[0:3, 1:36:3], 1.0), (T.cg[0:2, :], -1.0), (T.cg[0:2, 2:36:3], 1.0),
+                    (T.cg[0:1, :], 0.0), (T.cg[0:1, 0:36:3], 1.0)):
+        fc(ap, val)
+        V.wait_ge(S.vc, nv[0])
+    fc(T.m1[0:NB, :], 2.0 ** 23)
+    fc(T.m2[0:NB, :], 2.0 ** 23 - 0.5)
+    for e in order:
+        fc(T.st[0:3 * e + 3, e * 128:(e + 1) * 128], 1.0)
+    V.wait_ge(S.vc, nv[0])
+    for e in order:
+        if e:
+            fc(T.st[0:3 * e, e * 128:(e + 1) * 128], 0.0)
+    V.wait_ge(S.vc, nv[0])
+    V.wait_ge(S.ve, ne[0])
+
+    ph = [T.ph0, T.ph1, T.ph2, T.ph3]
+    pg = [T.pg0, T.pg1]
+
+    def col(n):
+        return slice(n * TOK, (n + 1) * TOK)
+
+    def mm_h(n):
+        e = order[n]
+        if e == r:
+            PE.wait_ge(S.ldo, 32)
+        elif e == sib:
+            PE.wait_ge(S["w%d" % e], bits(masks(topo, P, e)[1]))
+        else:
+            PE.wait_ge(S["w%d" % e], bits(topo.mask(P["landing"][(e, ci)], core)))
+        if n >= NHB:
+            PE.wait_ge(S.rl, n - NHB + 1)
+        PE.matmul(ph[n % NHB][:, :], T.wsb[:, e * 256:e * 256 + 128], T.xs[:, 0:TOK], True, True).then_inc(S.hm, 1)
+
+    def mm_g(n):
+        e = order[n]
+        if n >= 2:
+            PE.wait_ge(S.ml, n - 1)
+        PE.matmul(pg[n % 2][:, :], T.st[0:3 * e + 3, e * 128:(e + 1) * 128], T.gm[0:3 * e + 3, :], True, True).then_inc(S.gb, 1)
+
+    def mm_y(n):
+        e = order[n]
+        PE.wait_ge(S.ml, n + 1)
+        i = PE.matmul(T.py[:, :], T.wsb[:, e * 256 + 128:e * 256 + 256], T.hg[:, col(n)], n == 0, n == L - 1)
+        if n == L - 1:
+            i.then_inc(S.ym, 1)
+
+    PE.wait_ge(S.vc, nv[0])
+    PE.wait_ge(S.ldg, 16)
+    PE.matmul(T.pa[0:36, :], T.cg[0:3, :], T.gt[0:3, :], True, True).then_inc(S.dp, 1)
+    if boss:
+        PE.wait_ge(S.ldx, 48)
+    else:
+        PE.wait_ge(S.xa, bits(upper))
+    for n in range(pre):
+        mm_h(n)
+    PE.wait_ge(S.vs, sum(bits(topo.mask(h, core)) for h in P["paint"] if P["paint"][h][0] == r))
+    for q in range(NG):
+        PE.wait_ge(S.du, q)
+        PE.matmul(T.pg0[0:NB, q * NC:(q + 1) * NC], T.vt[32 * q:32 * q + 1, NC:NV], T.vt[32 * q:32 * q + 1, 0:NC],
+                  True, True).then_inc(S.du, 1)
+    PE.wait_ge(S.dm, 1)
+    PE.wait_ge(S.le, 16)
+    for h in range(2):
+        PE.matmul(T.pg1[0:36, h * NH:(h + 1) * NH], T.et[0:NB, 36 * h:36 * h + 36], T.ms[0:NB, :], True, True).then_inc(S.dq, 1)
+    PE.wait_ge(S.dg, 1)
+    mm_g(0)
+    mm_g(1)
+    for n in range(2 - pre):
+        mm_h(n)
+    for n in range(L):
+        if n + 2 < L:
+            mm_h(n + 2)
+        mm_y(n)
+        if n + 2 < L:
+            mm_g(n + 2)
+
+    def relu(n):
+        V.wait_ge(S.hm, n + 1)
+        V.tensor_tensor(out=T.hid[:, col(n)], in0=ph[n % NHB][:, :], in1=T.zt[:, :], op=A.max).then_inc(S.rl, 1)
+
+    def mult(n):
+        V.wait_ge(S.gb, n + 1)
+        V.wait_ge(S.rl, n + 1)
+        V.tensor_tensor(out=T.hg[:, col(n)], in0=T.hid[:, col(n)], in1=pg[n % 2][:, :], op=A.mult).then_inc(S.ml, 1)
+
+    for n in range(pre):
+        relu(n)
+    V.wait_ge(S.du, NG)
+    V.tensor_tensor(out=T.a1[0:NB, :], in0=T.pg0[0:NB, 0:NH], in1=T.m1[0:NB, :], op=A.add).then_inc(S.da, 1)
+    V.tensor_tensor(out=T.a2[0:NB, :], in0=T.pg0[0:NB, 0:NH], in1=T.m2[0:NB, :], op=A.add).then_inc(S.da, 1)
+    V.wait_ge(S.da, 2)
+    V.tensor_tensor(out=T.ms[0:NB, :], in0=T.a1[0:NB, :], in1=T.a2[0:NB, :], op=A.subtract).then_inc(S.dm, 1)
+    V.wait_ge(S.dq, 2)
+    V.tensor_tensor(out=T.tt[0:36, :], in0=T.pg1[0:36, :], in1=T.zt[0:36, :], op=A.max).then_inc(S.dt, 1)
+    V.wait_ge(S.dt, 1)
+    V.wait_ge(S.dp, 1)
+    V.tensor_tensor(out=T.gm[0:36, :], in0=T.tt[0:36, :], in1=T.pa[0:36, :], op=A.mult).then_inc(S.dg, 1)
+    for n in range(L):
+        if n >= pre:
+            relu(n)
+        mult(n)
+    V.wait_ge(S.ym, 1)
+    if boss and NA:
+        V.wait_ge(S.pp, bits(topo.mask(P["asst"][r], core)))
+        V.tensor_tensor(out=T.ysb[:, :], in0=T.py[:, :], in1=T.part[:, :], op=A.add).then_inc(S.yc, 1)
+    else:
+        V.tensor_copy(out=T.ysb[:, :], in_=T.py[:, :]).then_inc(S.yc, 1)
+    if boss:
+        SY.wait_ge(S.yc, 1)
+        SY.dma_start(T.y[:, :], T.ysb[:, :]).then_inc(S.st, 16)
+        SY.wait_ge(S.st, 16)
+    else:
+        g.wait_ge(S.yc, 1)
+        send(g, T, topo, core, [P["cores"][r]], T.part[:, :], T.ysb[:, :], S.pp, sent)
+    g.wait_ge(S.sent, sent[0])
+
+
+def rank_program(g, core, T, topo):
+    P = plan(T, topo)
+    rank = T.rank_of(core)
+    if rank is not None:
+        run_compute(g, core, rank, T, topo, P)
+    elif core in P["asst_of"]:
+        run_compute(g, core, P["asst_of"][core], T, topo, P)
+    elif core in P["paint"] or core in P["fan"] or core in P["relay_of"]:
+        run_helper(g, core, T, topo, P)

@@ -15,7 +15,7 @@ BIG = 4.0
 NSIM = 112
 ND = 3
 ARRIVE = [1, 2, 4, 3, 5]
-NA = 6
+NA = 4
 NHB = 4
 FAR = True
 
@@ -46,6 +46,12 @@ def values(route):
                     v |= 1 << (NE * h + e)
         out.append(v + 0.5)
     return out, [2.0 ** -(b + 1) for b in range(NB)]
+
+
+def parts(job):
+    a, b = job[1], job[2]
+    m = a + max(1, (b - a) // 4)
+    return [(a, m), (m, b)] if m < b else [(a, b)]
 
 
 def plan(T, topo):
@@ -140,16 +146,17 @@ def run_helper(g, core, T, topo, P):
     if job is not None:
         vals, scales = values(T.tables["ROUTE"][job[0]])
         n = 0
-        for c in range(job[1], job[2]):
-            if c < NC:
-                for q in range(NG):
-                    g.vector.memset(T.vt[32 * q:32 * q + 32, c:c + 1], vals[q * NC + c]).then_inc(S.pv, 1)
+        for a, b in parts(job):
+            for c in range(a, b):
+                if c < NC:
+                    for q in range(NG):
+                        g.vector.memset(T.vt[32 * q:32 * q + 32, c:c + 1], vals[q * NC + c]).then_inc(S.pv, 1)
+                        n += 1
+                else:
+                    g.vector.memset(T.vt[:, c:c + 1], scales[c - NC]).then_inc(S.pv, 1)
                     n += 1
-            else:
-                g.vector.memset(T.vt[:, c:c + 1], scales[c - NC]).then_inc(S.pv, 1)
-                n += 1
-        g.wait_ge(S.pv, n)
-        send(g, T, topo, core, team(P, job[0]), T.vt[:, job[1]:job[2]], T.vt[:, job[1]:job[2]], S.vs, sent)
+            g.wait_ge(S.pv, n)
+            send(g, T, topo, core, team(P, job[0]), T.vt[:, a:b], T.vt[:, a:b], S.vs, sent)
     r = P["relay_of"].get(core)
     if r is not None:
         ci = P["chips"].index(topo.chip(core))
@@ -291,7 +298,7 @@ def run_compute(g, core, r, T, topo, P):
         PE.wait_ge(S.xa, bits(upper))
     for n in range(pre):
         mm_h(n)
-    PE.wait_ge(S.vs, sum(bits(topo.mask(h, core)) for h in P["paint"] if P["paint"][h][0] == r))
+    PE.wait_ge(S.vs, sum(bits(topo.mask(h, core)) * len(parts(P["paint"][h])) for h in P["paint"] if P["paint"][h][0] == r))
     for q in range(NG):
         PE.wait_ge(S.du, q)
         PE.matmul(T.pg0[0:NB, q * NC:(q + 1) * NC], T.vt[32 * q:32 * q + 1, NC:NV], T.vt[32 * q:32 * q + 1, 0:NC],

@@ -1,6 +1,6 @@
 import numpy as np
 from concourse.bass import DstId, RemoteDMATransfer
-from concourse.mybir import AluOpType
+from concourse.mybir import AluOpType, ActivationFunctionType
 
 N = 12
 TOK = 512
@@ -10,25 +10,26 @@ NB = 2 * NE + 1
 NG = 4
 NC = NH // NG
 NV = NC + NB
-GX = 16
 BIG = 4.0
 NSIM = 112
 ND = 3
 ARRIVE = [1, 2, 4, 3, 5]
-NA = 4
+NT = 2
+RE = 2
+NA = 6
 NHB = 4
 FAR = True
 
 SCRATCH = {"wd": ("dram", [128, 256], "bfloat16"), "land": ("dram", [N, 128, 256], "bfloat16"),
-           "ef": ("sbuf", [128, 2, 828], "bfloat16")}
-for nm, w in (("xs", TOK + GX), ("part", TOK), ("wsb", N * 256), ("hid", N * TOK), ("hg", N * TOK), ("zt", TOK),
+           "gd": ("dram", [128, 3 * TOK // 128], "bfloat16"), "ef": ("sbuf", [128, 2, 828], "bfloat16")}
+for nm, w in (("xs", TOK), ("part", NT * TOK), ("wsb", N * 256), ("hid", N * TOK), ("hg", N * TOK),
               ("st", N * 128), ("ms", NH), ("et", 72), ("cg", 36), ("gt", TOK), ("tt", TOK), ("gm", TOK), ("ysb", TOK)):
     SCRATCH[nm] = ("sbuf", [128, w], "bfloat16")
-for nm, w in (("vt", NV), ("m1", NH), ("m2", NH), ("a1", NH), ("a2", NH)):
+for nm, w in (("vt", NV), ("a2", NH)):
     SCRATCH[nm] = ("sbuf", [128, w], "float32")
 for nm in ("py", "pa", "pg0", "pg1", "ph0", "ph1", "ph2", "ph3"):
     SCRATCH[nm] = ("psum", [128, TOK], "float32")
-SEMAPHORES = ["ldw", "ldx", "ldo", "ldg", "le", "st", "sent", "pv", "vs", "xa", "pp", "vc", "ve",
+SEMAPHORES = ["ldw", "ldx", "ldo", "ldg", "ldq", "ga", "le", "st", "sent", "pv", "vs", "xa", "pp0", "pp1", "vc", "ve",
               "hm", "rl", "gb", "ml", "ym", "yc", "du", "da", "dm", "dq", "dt", "dp", "dg"] + ["w%d" % e for e in range(N)]
 
 
@@ -63,24 +64,25 @@ def plan(T, topo):
     nc = len(chips)
     on = [[r for r in range(N) if topo.chip(cores[r]) == ch] for ch in chips]
     helpers = [[c for c in range(NSIM) if topo.chip(c) == ch and c not in cores] for ch in chips]
-    relay, relay_of, asst, asst_of, fans = {}, {}, {}, {}, []
+    relay, relay_of, asst, asst_of, fans, nd = {}, {}, {}, {}, [], {}
     fillers = [[] for r in range(N)]
     for i in range(nc):
         free = list(helpers[i])
         rel = []
-        for r in on[i]:
+        for q, r in enumerate(on[i]):
             cand = [h for h in free if topo.die(h) != topo.die(cores[r]) and all(topo.may_write(h, d) for d in cores)]
             relay[r] = cand[0]
             relay_of[cand[0]] = r
             rel.append(cand[0])
             free.remove(cand[0])
-        if NA:
+            nd[r] = ND - q % 2
+        for j in range(NT):
             for r in on[i]:
                 cand = [h for h in free if topo.die(h) == topo.die(cores[r])] + free
-                asst[r] = cand[0]
-                asst_of[cand[0]] = r
+                asst.setdefault(r, []).append(cand[0])
+                asst_of[cand[0]] = (r, j)
                 free.remove(cand[0])
-        fans.append(free + rel)
+        fans.append(rel)
         for q, h in enumerate(free + rel):
             fillers[on[i][q % len(on[i])]].append(h)
     if FAR:
@@ -102,16 +104,28 @@ def plan(T, topo):
             if b > a:
                 paint[h] = (r, a, b)
             a = b
-    order, landing, fan = [], {}, {}
+    order, landing, fan, target = [], {}, {}, {}
     for i in range(nc):
         arr = [e for k in ARRIVE for e in on[(i - k) % nc]]
         order.append(arr)
         for p, e in enumerate(arr):
-            h = fans[i][p % len(fans[i])]
+            if p < RE:
+                tg = [cores[q] for q in on[i]]
+                pool = [asst[q][(p // len(on[i])) % NT] for q in on[i]]
+                h = pool[p % len(pool)]
+            elif p < RE + NA:
+                j = (p - RE) % NT
+                tg = [asst[q][j] for q in on[i]]
+                pool = [asst[q][(j + 1) % NT] for q in on[i]]
+                h = pool[((p - RE) // NT) % len(pool)]
+            else:
+                tg = [cores[q] for q in on[i]]
+                h = fans[i][p % len(fans[i])]
             landing[(e, i)] = h
             fan.setdefault(h, []).append(e)
-    return {"cores": cores, "chips": chips, "on": on, "relay": relay, "relay_of": relay_of, "paint": paint,
-            "order": order, "landing": landing, "fan": fan, "nc": nc, "asst": asst, "asst_of": asst_of}
+            target[(e, h)] = tg
+    return {"cores": cores, "chips": chips, "on": on, "relay": relay, "relay_of": relay_of, "paint": paint, "nd": nd,
+            "order": order, "landing": landing, "fan": fan, "target": target, "nc": nc, "asst": asst, "asst_of": asst_of}
 
 
 def masks(topo, P, r):
@@ -120,10 +134,6 @@ def masks(topo, P, r):
     near = [d for d in P["cores"] if topo.chip(d) == topo.chip(c) and d != c][0]
     off = topo.mask(c, far)
     return off, topo.mask(c, near) & ~off
-
-
-def team(P, r):
-    return [P["cores"][r]] + ([P["asst"][r]] if NA else [])
 
 
 def did(topo, c):
@@ -137,6 +147,12 @@ def send(g, T, topo, src, dsts, out_ap, in_ap, rsem, sent, m=None):
     g.remote_dma_fused([RemoteDMATransfer(dst_ids=[did(topo, c) for c in dsts], dma_engine_mask=m, remote_sem=rsem,
                                           srcs=[in_ap], dsts=[out_ap for c in dsts], alu_op=0)], local_sem=T.sem.sent)
     sent[0] += bits(m)
+
+
+def run_fans(g, core, T, topo, P, sent):
+    for e in P["fan"].get(core, []):
+        g.wait_ge(T.sem["w%d" % e], bits(topo.mask(P["cores"][e], core)))
+        send(g, T, topo, core, P["target"][(e, core)], T.wsb[:, e * 256:(e + 1) * 256], T.land[e], T.sem["w%d" % e], sent)
 
 
 def run_helper(g, core, T, topo, P):
@@ -156,42 +172,41 @@ def run_helper(g, core, T, topo, P):
                     g.vector.memset(T.vt[:, c:c + 1], scales[c - NC]).then_inc(S.pv, 1)
                     n += 1
             g.wait_ge(S.pv, n)
-            send(g, T, topo, core, team(P, job[0]), T.vt[:, a:b], T.vt[:, a:b], S.vs, sent)
+            send(g, T, topo, core, [P["cores"][job[0]]], T.vt[:, a:b], T.vt[:, a:b], S.vs, sent)
     r = P["relay_of"].get(core)
     if r is not None:
         ci = P["chips"].index(topo.chip(core))
         g.wait_ge(S["w%d" % r], bits(masks(topo, P, r)[1]))
-        for k in range(ND + 1, P["nc"]):
-            send(g, T, topo, core, [P["landing"][(r, (ci + k) % P["nc"])]], T.land[r], T.land[r], S["w%d" % r], sent)
-    for e in P["fan"].get(core, []):
-        ci = P["chips"].index(topo.chip(core))
-        g.wait_ge(S["w%d" % e], bits(topo.mask(P["cores"][e], core)))
-        early = P["order"][ci].index(e) < NA
-        tg = [P["asst"][q] if early else P["cores"][q] for q in P["on"][ci]]
-        send(g, T, topo, core, tg, T.wsb[:, e * 256:(e + 1) * 256], T.land[e], S["w%d" % e], sent)
+        for k in ARRIVE:
+            if k > P["nd"][r]:
+                send(g, T, topo, core, [P["landing"][(r, (ci + k) % P["nc"])]], T.land[r], T.land[r], S["w%d" % r], sent)
+    run_fans(g, core, T, topo, P, sent)
     g.wait_ge(S.sent, sent[0])
 
 
-def run_compute(g, core, r, T, topo, P):
+def run_compute(g, core, r, j, T, topo, P):
     S = T.sem
     V, PE, SY, SC = g.vector, g.tensor, g.sync, g.scalar
     ci = P["chips"].index(topo.chip(core))
     nc = P["nc"]
-    boss = core == P["cores"][r]
+    boss = j is None
     sib = [q for q in P["on"][ci] if q != r][0]
-    order = ([r, sib] + P["order"][ci][NA:]) if boss else P["order"][ci][:NA]
+    arr = P["order"][ci]
+    order = ([r, sib] + arr[:RE] + arr[RE + NA:]) if boss else arr[RE + j:RE + NA:NT]
     L = len(order)
-    pre = 2 if boss else 0
     off, upper = masks(topo, P, r)
     A = AluOpType
     sent = [0]
+    if boss:
+        nvs = sum(bits(topo.mask(h, core)) * len(parts(P["paint"][h])) for h in P["paint"] if P["paint"][h][0] == r)
+    else:
+        nvs = bits(topo.mask(P["cores"][r], core))
 
     if boss:
         SY.dma_start(T.wd[:, 0:128], T.w1[:, :]).then_inc(S.ldw, 16)
         SC.dma_start(T.wd[:, 128:256], T.w2[:, :]).then_inc(S.ldw, 16)
-        SY.dma_start(T.xs[:, 0:TOK], T.x[:, :]).then_inc(S.ldx, 16)
-        SC.dma_start(T.xs[0:96, TOK:TOK + GX], T.gate[:, :]).then_inc(S.ldx, 16)
-        SC.dma_start(T.xs[96:128, TOK:TOK + GX], T.gate[0:1, :]).then_inc(S.ldx, 16)
+        SC.dma_start(T.gd[:, :], T.gate[:, :]).then_inc(S.ldq, 16)
+        SY.dma_start(T.xs[:, :], T.x[:, :]).then_inc(S.ldx, 16)
         SC.dma_start(T.wsb[:, r * 256 + 128:r * 256 + 256], T.w2[:, :]).then_inc(S.ldo, 16)
         SY.dma_start(T.wsb[:, r * 256:r * 256 + 128], T.w1[:, :]).then_inc(S.ldo, 16)
         SC.dma_start(T.gt[0:3, :], T.gate[:, :]).then_inc(S.ldg, 16)
@@ -204,15 +219,18 @@ def run_compute(g, core, r, T, topo, P):
                               remote_sem=wsem, srcs=[T.wd[:, :]],
                               dsts=[T.land[r], T.wsb[:, r * 256:(r + 1) * 256]], alu_op=0)], local_sem=S.sent)
         sent[0] += bits(off) + bits(upper)
-        for k in range(2, ND + 1):
+        g.wait_ge(S.ldq, 16)
+        send(g, T, topo, core, P["asst"][r], T.gd[:, :], T.gd[:, :], S.ga, sent, upper)
+        for k in range(2, P["nd"][r] + 1):
             send(g, T, topo, core, [P["landing"][(r, (ci + k) % nc)]], T.land[r], T.wd[:, :], wsem, sent)
             if k == 2:
-                g.wait_ge(S.ldx, 48)
-                if NA:
-                    send(g, T, topo, core, [P["asst"][r]], T.xs[:, :], T.xs[:, :], S.xa, sent, upper)
+                g.wait_ge(S.ldx, 16)
+                send(g, T, topo, core, P["asst"][r], T.xs[:, :], T.xs[:, :], S.xa, sent, upper)
+        g.wait_ge(S.vs, nvs)
+        send(g, T, topo, core, P["asst"][r], T.vt[:, :], T.vt[:, :], S.vs, sent)
     else:
-        SY.wait_ge(S.xa, bits(upper))
-        SY.dma_start(T.gt[0:3, :], T.xs[0:96, TOK:TOK + GX]).then_inc(S.ldg, 16)
+        SY.wait_ge(S.ga, bits(upper))
+        SY.dma_start(T.gt[0:3, :], T.gd[:, :]).then_inc(S.ldg, 16)
 
     nv, ne = [0], [0]
 
@@ -224,7 +242,6 @@ def run_compute(g, core, r, T, topo, P):
         V.memset(ap, val).then_inc(S.ve, 1)
         ne[0] += 1
 
-    fc(T.zt[:, :], 0.0)
     fe(T.ef[0:1, :, :], 0.0)
     V.wait_ge(S.ve, ne[0])
     for k in range(3):
@@ -247,8 +264,6 @@ def run_compute(g, core, r, T, topo, P):
                     (T.cg[0:1, :], 0.0), (T.cg[0:1, 0:36:3], 1.0)):
         fc(ap, val)
         V.wait_ge(S.vc, nv[0])
-    fc(T.m1[0:NB, :], 2.0 ** 23)
-    fc(T.m2[0:NB, :], 2.0 ** 23 - 0.5)
     for e in order:
         fc(T.st[0:3 * e + 3, e * 128:(e + 1) * 128], 1.0)
     V.wait_ge(S.vc, nv[0])
@@ -264,6 +279,8 @@ def run_compute(g, core, r, T, topo, P):
     def col(n):
         return slice(n * TOK, (n + 1) * TOK)
 
+    nh = [0]
+
     def mm_h(n):
         e = order[n]
         if e == r:
@@ -274,7 +291,12 @@ def run_compute(g, core, r, T, topo, P):
             PE.wait_ge(S["w%d" % e], bits(topo.mask(P["landing"][(e, ci)], core)))
         if n >= NHB:
             PE.wait_ge(S.rl, n - NHB + 1)
-        PE.matmul(ph[n % NHB][:, :], T.wsb[:, e * 256:e * 256 + 128], T.xs[:, 0:TOK], True, True).then_inc(S.hm, 1)
+        PE.matmul(ph[n % NHB][:, :], T.wsb[:, e * 256:e * 256 + 128], T.xs[:, :], True, True).then_inc(S.hm, 1)
+
+    def h_upto(k):
+        while nh[0] < min(k, L):
+            mm_h(nh[0])
+            nh[0] += 1
 
     def mm_g(n):
         e = order[n]
@@ -293,70 +315,72 @@ def run_compute(g, core, r, T, topo, P):
     PE.wait_ge(S.ldg, 16)
     PE.matmul(T.pa[0:36, :], T.cg[0:3, :], T.gt[0:3, :], True, True).then_inc(S.dp, 1)
     if boss:
-        PE.wait_ge(S.ldx, 48)
-    else:
-        PE.wait_ge(S.xa, bits(upper))
-    for n in range(pre):
-        mm_h(n)
-    PE.wait_ge(S.vs, sum(bits(topo.mask(h, core)) * len(parts(P["paint"][h])) for h in P["paint"] if P["paint"][h][0] == r))
+        PE.wait_ge(S.ldx, 16)
+        h_upto(2)
+    PE.wait_ge(S.vs, nvs)
     for q in range(NG):
         PE.wait_ge(S.du, q)
         PE.matmul(T.pg0[0:NB, q * NC:(q + 1) * NC], T.vt[32 * q:32 * q + 1, NC:NV], T.vt[32 * q:32 * q + 1, 0:NC],
                   True, True).then_inc(S.du, 1)
+    if boss:
+        h_upto(2 + RE)
+    else:
+        PE.wait_ge(S.xa, bits(upper))
+        h_upto(2)
     PE.wait_ge(S.dm, 1)
     PE.wait_ge(S.le, 16)
     for h in range(2):
         PE.matmul(T.pg1[0:36, h * NH:(h + 1) * NH], T.et[0:NB, 36 * h:36 * h + 36], T.ms[0:NB, :], True, True).then_inc(S.dq, 1)
+    if not boss:
+        h_upto(3)
     PE.wait_ge(S.dg, 1)
     mm_g(0)
     mm_g(1)
-    for n in range(2 - pre):
-        mm_h(n)
     for n in range(L):
-        if n + 2 < L:
-            mm_h(n + 2)
+        h_upto(n + 3)
         mm_y(n)
         if n + 2 < L:
             mm_g(n + 2)
 
-    def relu(n):
-        V.wait_ge(S.hm, n + 1)
-        V.tensor_tensor(out=T.hid[:, col(n)], in0=ph[n % NHB][:, :], in1=T.zt[:, :], op=A.max).then_inc(S.rl, 1)
+    for n in range(L):
+        SC.wait_ge(S.hm, n + 1)
+        SC.activation(out=T.hid[:, col(n)], in_=ph[n % NHB][:, :], func=ActivationFunctionType.Relu).then_inc(S.rl, 1)
 
     def mult(n):
         V.wait_ge(S.gb, n + 1)
         V.wait_ge(S.rl, n + 1)
         V.tensor_tensor(out=T.hg[:, col(n)], in0=T.hid[:, col(n)], in1=pg[n % 2][:, :], op=A.mult).then_inc(S.ml, 1)
 
-    for n in range(pre):
-        relu(n)
+    a1 = T.pg0[0:NB, NH:2 * NH]
     V.wait_ge(S.du, NG)
-    V.tensor_tensor(out=T.a1[0:NB, :], in0=T.pg0[0:NB, 0:NH], in1=T.m1[0:NB, :], op=A.add).then_inc(S.da, 1)
-    V.tensor_tensor(out=T.a2[0:NB, :], in0=T.pg0[0:NB, 0:NH], in1=T.m2[0:NB, :], op=A.add).then_inc(S.da, 1)
+    V.tensor_scalar(out=a1, in0=T.pg0[0:NB, 0:NH], scalar1=2.0 ** 23, scalar2=None, op0=A.add).then_inc(S.da, 1)
+    V.tensor_scalar(out=T.a2[0:NB, :], in0=T.pg0[0:NB, 0:NH], scalar1=2.0 ** 23 - 0.5, scalar2=None, op0=A.add).then_inc(S.da, 1)
     V.wait_ge(S.da, 2)
-    V.tensor_tensor(out=T.ms[0:NB, :], in0=T.a1[0:NB, :], in1=T.a2[0:NB, :], op=A.subtract).then_inc(S.dm, 1)
+    V.tensor_tensor(out=T.ms[0:NB, :], in0=a1, in1=T.a2[0:NB, :], op=A.subtract).then_inc(S.dm, 1)
     V.wait_ge(S.dq, 2)
-    V.tensor_tensor(out=T.tt[0:36, :], in0=T.pg1[0:36, :], in1=T.zt[0:36, :], op=A.max).then_inc(S.dt, 1)
+    V.tensor_scalar(out=T.tt[0:36, :], in0=T.pg1[0:36, :], scalar1=0.0, scalar2=None, op0=A.max).then_inc(S.dt, 1)
     V.wait_ge(S.dt, 1)
     V.wait_ge(S.dp, 1)
     V.tensor_tensor(out=T.gm[0:36, :], in0=T.tt[0:36, :], in1=T.pa[0:36, :], op=A.mult).then_inc(S.dg, 1)
     for n in range(L):
-        if n >= pre:
-            relu(n)
         mult(n)
     V.wait_ge(S.ym, 1)
-    if boss and NA:
-        V.wait_ge(S.pp, bits(topo.mask(P["asst"][r], core)))
-        V.tensor_tensor(out=T.ysb[:, :], in0=T.py[:, :], in1=T.part[:, :], op=A.add).then_inc(S.yc, 1)
+    if boss:
+        V.wait_ge(S.pp0, bits(topo.mask(P["asst"][r][0], core)))
+        V.tensor_tensor(out=T.py[:, :], in0=T.py[:, :], in1=T.part[:, 0:TOK], op=A.add).then_inc(S.yc, 1)
+        V.wait_ge(S.yc, 1)
+        V.wait_ge(S.pp1, bits(topo.mask(P["asst"][r][1], core)))
+        V.tensor_tensor(out=T.ysb[:, :], in0=T.py[:, :], in1=T.part[:, TOK:2 * TOK], op=A.add).then_inc(S.yc, 1)
     else:
         V.tensor_copy(out=T.ysb[:, :], in_=T.py[:, :]).then_inc(S.yc, 1)
     if boss:
-        SY.wait_ge(S.yc, 1)
+        SY.wait_ge(S.yc, 2)
         SY.dma_start(T.y[:, :], T.ysb[:, :]).then_inc(S.st, 16)
         SY.wait_ge(S.st, 16)
     else:
+        run_fans(g, core, T, topo, P, sent)
         g.wait_ge(S.yc, 1)
-        send(g, T, topo, core, [P["cores"][r]], T.part[:, :], T.ysb[:, :], S.pp, sent)
+        send(g, T, topo, core, [P["cores"][r]], T.part[:, j * TOK:(j + 1) * TOK], T.ysb[:, :], S["pp%d" % j], sent)
     g.wait_ge(S.sent, sent[0])
 
 
@@ -364,8 +388,8 @@ def rank_program(g, core, T, topo):
     P = plan(T, topo)
     rank = T.rank_of(core)
     if rank is not None:
-        run_compute(g, core, rank, T, topo, P)
+        run_compute(g, core, rank, None, T, topo, P)
     elif core in P["asst_of"]:
-        run_compute(g, core, P["asst_of"][core], T, topo, P)
+        run_compute(g, core, P["asst_of"][core][0], P["asst_of"][core][1], T, topo, P)
     elif core in P["paint"] or core in P["fan"] or core in P["relay_of"]:
         run_helper(g, core, T, topo, P)

import numpy as np
from concourse.bass import DstId, RemoteDMATransfer
from concourse.mybir import AluOpType, ActivationFunctionType

N = 12
TOK = 512
NH = TOK // 2
NE = 11
NB = 2 * NE + 1
NG = 4
NC = NH // NG
NV = NC + NB
BIG = 4.0
NSIM = 112
ND = 3
ARRIVE = [1, 2, 4, 3, 5]
NT = 2
RE = 2
NA = 6
NHB = 4
FAR = True

SCRATCH = {"wd": ("dram", [128, 256], "bfloat16"), "land": ("dram", [N, 128, 256], "bfloat16"),
           "gd": ("dram", [128, 3 * TOK // 128], "bfloat16"), "ef": ("sbuf", [128, 2, 828], "bfloat16")}
for nm, w in (("xs", TOK), ("part", NT * TOK), ("wsb", N * 256), ("hid", N * TOK), ("hg", N * TOK),
              ("st", N * 128), ("ms", NH), ("et", 72), ("cg", 36), ("gt", TOK), ("tt", TOK), ("gm", TOK), ("ysb", TOK)):
    SCRATCH[nm] = ("sbuf", [128, w], "bfloat16")
for nm, w in (("vt", NV), ("a2", NH)):
    SCRATCH[nm] = ("sbuf", [128, w], "float32")
for nm in ("py", "pa", "pg0", "pg1", "ph0", "ph1", "ph2", "ph3"):
    SCRATCH[nm] = ("psum", [128, TOK], "float32")
SEMAPHORES = ["ldw", "ldx", "ldo", "ldg", "ldq", "ga", "le", "st", "sent", "pv", "vs", "xa", "pp0", "pp1", "vc", "ve",
              "hm", "rl", "gb", "ml", "ym", "yc", "du", "da", "dm", "dq", "dt", "dp", "dg"] + ["w%d" % e for e in range(N)]


def bits(m):
    return bin(m).count("1")


def values(route):
    out = []
    for j in range(NH):
        v = 1 << (2 * NE)
        for h in range(2):
            for e in route[h * NH + j]:
                if e < NE:
                    v |= 1 << (NE * h + e)
        out.append(v + 0.5)
    return out, [2.0 ** -(b + 1) for b in range(NB)]


def parts(job):
    a, b = job[1], job[2]
    m = a + max(1, (b - a) // 4)
    return [(a, m), (m, b)] if m < b else [(a, b)]


def plan(T, topo):
    cores = list(T.cores)
    chips = []
    for c in cores:
        if topo.chip(c) not in chips:
            chips.append(topo.chip(c))
    nc = len(chips)
    on = [[r for r in range(N) if topo.chip(cores[r]) == ch] for ch in chips]
    helpers = [[c for c in range(NSIM) if topo.chip(c) == ch and c not in cores] for ch in chips]
    relay, relay_of, asst, asst_of, fans, nd = {}, {}, {}, {}, [], {}
    fillers = [[] for r in range(N)]
    for i in range(nc):
        free = list(helpers[i])
        rel = []
        for q, r in enumerate(on[i]):
            cand = [h for h in free if topo.die(h) != topo.die(cores[r]) and all(topo.may_write(h, d) for d in cores)]
            relay[r] = cand[0]
            relay_of[cand[0]] = r
            rel.append(cand[0])
            free.remove(cand[0])
            nd[r] = ND - q % 2
        for j in range(NT):
            for r in on[i]:
                cand = [h for h in free if topo.die(h) == topo.die(cores[r])] + free
                asst.setdefault(r, []).append(cand[0])
                asst_of[cand[0]] = (r, j)
                free.remove(cand[0])
        fans.append(rel)
        for q, h in enumerate(free + rel):
            fillers[on[i][q % len(on[i])]].append(h)
    if FAR:
        idle = [c for c in range(NSIM) if topo.chip(c) not in chips]
        idle.sort(key=lambda c: sum(1 for d in cores if topo.may_write(c, d)))
        for c in idle:
            ok = [r for r in range(N) if topo.may_write(c, cores[r])]
            r = min(ok, key=lambda q: len(fillers[q]))
            fillers[r].append(c)
    paint = {}
    wt = [NG] * NC + [1] * NB
    for r in range(N):
        k, a, acc, tot = len(fillers[r]), 0, 0, sum(wt)
        for s, h in enumerate(fillers[r]):
            b = a
            while b < NV and (s == k - 1 or acc + wt[b] <= tot * (s + 1) / k + 1e-9):
                acc += wt[b]
                b += 1
            if b > a:
                paint[h] = (r, a, b)
            a = b
    order, landing, fan, target = [], {}, {}, {}
    for i in range(nc):
        arr = [e for k in ARRIVE for e in on[(i - k) % nc]]
        order.append(arr)
        for p, e in enumerate(arr):
            if p < RE:
                tg = [cores[q] for q in on[i]]
                pool = [asst[q][(p // len(on[i])) % NT] for q in on[i]]
                h = pool[p % len(pool)]
            elif p < RE + NA:
                j = (p - RE) % NT
                tg = [asst[q][j] for q in on[i]]
                pool = [asst[q][(j + 1) % NT] for q in on[i]]
                h = pool[((p - RE) // NT) % len(pool)]
            else:
                tg = [cores[q] for q in on[i]]
                h = fans[i][p % len(fans[i])]
            landing[(e, i)] = h
            fan.setdefault(h, []).append(e)
            target[(e, h)] = tg
    return {"cores": cores, "chips": chips, "on": on, "relay": relay, "relay_of": relay_of, "paint": paint, "nd": nd,
            "order": order, "landing": landing, "fan": fan, "target": target, "nc": nc, "asst": asst, "asst_of": asst_of}


def masks(topo, P, r):
    c = P["cores"][r]
    far = [d for d in P["cores"] if topo.chip(d) != topo.chip(c)][0]
    near = [d for d in P["cores"] if topo.chip(d) == topo.chip(c) and d != c][0]
    off = topo.mask(c, far)
    return off, topo.mask(c, near) & ~off


def did(topo, c):
    rid, pid, se = topo.addr(c)
    return DstId(rid=rid, pnc=pid)


def send(g, T, topo, src, dsts, out_ap, in_ap, rsem, sent, m=None):
    if m is None:
        m = topo.mask(src, dsts[0])
    g.remote_dma_fused([RemoteDMATransfer(dst_ids=[did(topo, c) for c in dsts], dma_engine_mask=m, remote_sem=rsem,
                                          srcs=[in_ap], dsts=[out_ap for c in dsts], alu_op=0)], local_sem=T.sem.sent)
    sent[0] += bits(m)


def run_fans(g, core, T, topo, P, sent):
    for e in P["fan"].get(core, []):
        g.wait_ge(T.sem["w%d" % e], bits(topo.mask(P["cores"][e], core)))
        send(g, T, topo, core, P["target"][(e, core)], T.wsb[:, e * 256:(e + 1) * 256], T.land[e], T.sem["w%d" % e], sent)


def run_helper(g, core, T, topo, P):
    sent = [0]
    S = T.sem
    job = P["paint"].get(core)
    if job is not None:
        vals, scales = values(T.tables["ROUTE"][job[0]])
        n = 0
        for a, b in parts(job):
            for c in range(a, b):
                if c < NC:
                    for q in range(NG):
                        g.vector.memset(T.vt[32 * q:32 * q + 32, c:c + 1], vals[q * NC + c]).then_inc(S.pv, 1)
                        n += 1
                else:
                    g.vector.memset(T.vt[:, c:c + 1], scales[c - NC]).then_inc(S.pv, 1)
                    n += 1
            g.wait_ge(S.pv, n)
            send(g, T, topo, core, [P["cores"][job[0]]], T.vt[:, a:b], T.vt[:, a:b], S.vs, sent)
    r = P["relay_of"].get(core)
    if r is not None:
        ci = P["chips"].index(topo.chip(core))
        g.wait_ge(S["w%d" % r], bits(masks(topo, P, r)[1]))
        for k in ARRIVE:
            if k > P["nd"][r]:
                send(g, T, topo, core, [P["landing"][(r, (ci + k) % P["nc"])]], T.land[r], T.land[r], S["w%d" % r], sent)
    run_fans(g, core, T, topo, P, sent)
    g.wait_ge(S.sent, sent[0])


def run_compute(g, core, r, j, T, topo, P):
    S = T.sem
    V, PE, SY, SC = g.vector, g.tensor, g.sync, g.scalar
    ci = P["chips"].index(topo.chip(core))
    nc = P["nc"]
    boss = j is None
    sib = [q for q in P["on"][ci] if q != r][0]
    arr = P["order"][ci]
    order = ([r, sib] + arr[:RE] + arr[RE + NA:]) if boss else arr[RE + j:RE + NA:NT]
    L = len(order)
    off, upper = masks(topo, P, r)
    A = AluOpType
    sent = [0]
    if boss:
        nvs = sum(bits(topo.mask(h, core)) * len(parts(P["paint"][h])) for h in P["paint"] if P["paint"][h][0] == r)
    else:
        nvs = bits(topo.mask(P["cores"][r], core))

    if boss:
        SY.dma_start(T.wd[:, 0:128], T.w1[:, :]).then_inc(S.ldw, 16)
        SC.dma_start(T.wd[:, 128:256], T.w2[:, :]).then_inc(S.ldw, 16)
        SC.dma_start(T.gd[:, :], T.gate[:, :]).then_inc(S.ldq, 16)
        SY.dma_start(T.xs[:, :], T.x[:, :]).then_inc(S.ldx, 16)
        SC.dma_start(T.wsb[:, r * 256 + 128:r * 256 + 256], T.w2[:, :]).then_inc(S.ldo, 16)
        SY.dma_start(T.wsb[:, r * 256:r * 256 + 128], T.w1[:, :]).then_inc(S.ldo, 16)
        SC.dma_start(T.gt[0:3, :], T.gate[:, :]).then_inc(S.ldg, 16)
        wsem = S["w%d" % r]
        g.wait_ge(S.ldw, 32)
        g.remote_dma_fused([
            RemoteDMATransfer(dst_ids=[did(topo, P["landing"][(r, (ci + 1) % nc)])], dma_engine_mask=off, remote_sem=wsem,
                              srcs=[T.wd[:, :]], dsts=[T.land[r]], alu_op=0),
            RemoteDMATransfer(dst_ids=[did(topo, P["relay"][r]), did(topo, P["cores"][sib])], dma_engine_mask=upper,
                              remote_sem=wsem, srcs=[T.wd[:, :]],
                              dsts=[T.land[r], T.wsb[:, r * 256:(r + 1) * 256]], alu_op=0)], local_sem=S.sent)
        sent[0] += bits(off) + bits(upper)
        g.wait_ge(S.ldq, 16)
        send(g, T, topo, core, P["asst"][r], T.gd[:, :], T.gd[:, :], S.ga, sent, upper)
        for k in range(2, P["nd"][r] + 1):
            send(g, T, topo, core, [P["landing"][(r, (ci + k) % nc)]], T.land[r], T.wd[:, :], wsem, sent)
            if k == 2:
                g.wait_ge(S.ldx, 16)
                send(g, T, topo, core, P["asst"][r], T.xs[:, :], T.xs[:, :], S.xa, sent, upper)
        g.wait_ge(S.vs, nvs)
        send(g, T, topo, core, P["asst"][r], T.vt[:, :], T.vt[:, :], S.vs, sent)
    else:
        SY.wait_ge(S.ga, bits(upper))
        SY.dma_start(T.gt[0:3, :], T.gd[:, :]).then_inc(S.ldg, 16)

    nv, ne = [0], [0]

    def fc(ap, val):
        V.memset(ap, val).then_inc(S.vc, 1)
        nv[0] += 1

    def fe(ap, val):
        V.memset(ap, val).then_inc(S.ve, 1)
        ne[0] += 1

    fe(T.ef[0:1, :, :], 0.0)
    V.wait_ge(S.ve, ne[0])
    for k in range(3):
        fe(T.ef[0:1, :, k:k + 751:75], BIG if k < 2 else 1.0)
    for e1 in range(NE - 1):
        for k in range(2):
            a = 72 * e1 + 3 * (e1 + 1) + k
            fe(T.ef[0:1, :, a:a + 3 * (NE - 2 - e1) + 1:3], -1.0 if k == 0 else 1.0)
    for k in (1, 2):
        fe(T.ef[0:1, :, 33 + k:33 + k + 721:72], -1.0)
    fe(T.ef[0:1, 1, 756:756 + 70:3], 1.0 - BIG)
    fe(T.ef[0:1, 1, 757:757 + 70:3], -1.0 - BIG)
    V.wait_ge(S.ve, ne[0])
    fe(T.ef[0:1, 1, 756 + 33:756 + 70:36], 0.0)
    fe(T.ef[0:1, 1, 756 + 34:756 + 36], 3.0)
    fe(T.ef[0:1, 1, 756 + 70:756 + 72], 3.0)
    SY.wait_ge(S.ve, ne[0])
    SY.dma_start(T.et[0:NB, :], T.ef[0:1, :, :]).then_inc(S.le, 16)
    for ap, val in ((T.cg[0:3, :], 0.0), (T.cg[0:3, 1:36:3], 1.0), (T.cg[0:2, :], -1.0), (T.cg[0:2, 2:36:3], 1.0),
                    (T.cg[0:1, :], 0.0), (T.cg[0:1, 0:36:3], 1.0)):
        fc(ap, val)
        V.wait_ge(S.vc, nv[0])
    for e in order:
        fc(T.st[0:3 * e + 3, e * 128:(e + 1) * 128], 1.0)
    V.wait_ge(S.vc, nv[0])
    for e in order:
        if e:
            fc(T.st[0:3 * e, e * 128:(e + 1) * 128], 0.0)
    V.wait_ge(S.vc, nv[0])
    V.wait_ge(S.ve, ne[0])

    ph = [T.ph0, T.ph1, T.ph2, T.ph3]
    pg = [T.pg0, T.pg1]

    def col(n):
        return slice(n * TOK, (n + 1) * TOK)

    nh = [0]

    def mm_h(n):
        e = order[n]
        if e == r:
            PE.wait_ge(S.ldo, 32)
        elif e == sib:
            PE.wait_ge(S["w%d" % e], bits(masks(topo, P, e)[1]))
        else:
            PE.wait_ge(S["w%d" % e], bits(topo.mask(P["landing"][(e, ci)], core)))
        if n >= NHB:
            PE.wait_ge(S.rl, n - NHB + 1)
        PE.matmul(ph[n % NHB][:, :], T.wsb[:, e * 256:e * 256 + 128], T.xs[:, :], True, True).then_inc(S.hm, 1)

    def h_upto(k):
        while nh[0] < min(k, L):
            mm_h(nh[0])
            nh[0] += 1

    def mm_g(n):
        e = order[n]
        if n >= 2:
            PE.wait_ge(S.ml, n - 1)
        PE.matmul(pg[n % 2][:, :], T.st[0:3 * e + 3, e * 128:(e + 1) * 128], T.gm[0:3 * e + 3, :], True, True).then_inc(S.gb, 1)

    def mm_y(n):
        e = order[n]
        PE.wait_ge(S.ml, n + 1)
        i = PE.matmul(T.py[:, :], T.wsb[:, e * 256 + 128:e * 256 + 256], T.hg[:, col(n)], n == 0, n == L - 1)
        if n == L - 1:
            i.then_inc(S.ym, 1)

    PE.wait_ge(S.vc, nv[0])
    PE.wait_ge(S.ldg, 16)
    PE.matmul(T.pa[0:36, :], T.cg[0:3, :], T.gt[0:3, :], True, True).then_inc(S.dp, 1)
    if boss:
        PE.wait_ge(S.ldx, 16)
        h_upto(2)
    PE.wait_ge(S.vs, nvs)
    for q in range(NG):
        PE.wait_ge(S.du, q)
        PE.matmul(T.pg0[0:NB, q * NC:(q + 1) * NC], T.vt[32 * q:32 * q + 1, NC:NV], T.vt[32 * q:32 * q + 1, 0:NC],
                  True, True).then_inc(S.du, 1)
    if boss:
        h_upto(2 + RE)
    else:
        PE.wait_ge(S.xa, bits(upper))
        h_upto(2)
    PE.wait_ge(S.dm, 1)
    PE.wait_ge(S.le, 16)
    for h in range(2):
        PE.matmul(T.pg1[0:36, h * NH:(h + 1) * NH], T.et[0:NB, 36 * h:36 * h + 36], T.ms[0:NB, :], True, True).then_inc(S.dq, 1)
    if not boss:
        h_upto(3)
    PE.wait_ge(S.dg, 1)
    mm_g(0)
    mm_g(1)
    for n in range(L):
        h_upto(n + 3)
        mm_y(n)
        if n + 2 < L:
            mm_g(n + 2)

    for n in range(L):
        SC.wait_ge(S.hm, n + 1)
        SC.activation(out=T.hid[:, col(n)], in_=ph[n % NHB][:, :], func=ActivationFunctionType.Relu).then_inc(S.rl, 1)

    def mult(n):
        V.wait_ge(S.gb, n + 1)
        V.wait_ge(S.rl, n + 1)
        V.tensor_tensor(out=T.hg[:, col(n)], in0=T.hid[:, col(n)], in1=pg[n % 2][:, :], op=A.mult).then_inc(S.ml, 1)

    a1 = T.pg0[0:NB, NH:2 * NH]
    V.wait_ge(S.du, NG)
    V.tensor_scalar(out=a1, in0=T.pg0[0:NB, 0:NH], scalar1=2.0 ** 23, scalar2=None, op0=A.add).then_inc(S.da, 1)
    V.tensor_scalar(out=T.a2[0:NB, :], in0=T.pg0[0:NB, 0:NH], scalar1=2.0 ** 23 - 0.5, scalar2=None, op0=A.add).then_inc(S.da, 1)
    V.wait_ge(S.da, 2)
    V.tensor_tensor(out=T.ms[0:NB, :], in0=a1, in1=T.a2[0:NB, :], op=A.subtract).then_inc(S.dm, 1)
    V.wait_ge(S.dq, 2)
    V.tensor_scalar(out=T.tt[0:36, :], in0=T.pg1[0:36, :], scalar1=0.0, scalar2=None, op0=A.max).then_inc(S.dt, 1)
    V.wait_ge(S.dt, 1)
    V.wait_ge(S.dp, 1)
    V.tensor_tensor(out=T.gm[0:36, :], in0=T.tt[0:36, :], in1=T.pa[0:36, :], op=A.mult).then_inc(S.dg, 1)
    for n in range(L):
        mult(n)
    V.wait_ge(S.ym, 1)
    if boss:
        V.wait_ge(S.pp0, bits(topo.mask(P["asst"][r][0], core)))
        V.tensor_tensor(out=T.py[:, :], in0=T.py[:, :], in1=T.part[:, 0:TOK], op=A.add).then_inc(S.yc, 1)
        V.wait_ge(S.yc, 1)
        V.wait_ge(S.pp1, bits(topo.mask(P["asst"][r][1], core)))
        V.tensor_tensor(out=T.ysb[:, :], in0=T.py[:, :], in1=T.part[:, TOK:2 * TOK], op=A.add).then_inc(S.yc, 1)
    else:
        V.tensor_copy(out=T.ysb[:, :], in_=T.py[:, :]).then_inc(S.yc, 1)
    if boss:
        SY.wait_ge(S.yc, 2)
        SY.dma_start(T.y[:, :], T.ysb[:, :]).then_inc(S.st, 16)
        SY.wait_ge(S.st, 16)
    else:
        run_fans(g, core, T, topo, P, sent)
        g.wait_ge(S.yc, 1)
        send(g, T, topo, core, [P["cores"][r]], T.part[:, j * TOK:(j + 1) * TOK], T.ysb[:, :], S["pp%d" % j], sent)
    g.wait_ge(S.sent, sent[0])


def rank_program(g, core, T, topo):
    P = plan(T, topo)
    rank = T.rank_of(core)
    if rank is not None:
        run_compute(g, core, rank, None, T, topo, P)
    elif core in P["asst_of"]:
        run_compute(g, core, P["asst_of"][core][0], P["asst_of"][core][1], T, topo, P)
    elif core in P["paint"] or core in P["fan"] or core in P["relay_of"]:
        run_helper(g, core, T, topo, P)
